import numpy as np
import ml_dtypes


def mxq(x, axis, fmt="e4m3"):
    dtype, down = {"e4m3": (ml_dtypes.float8_e4m3fn, 7), "e5m2": (ml_dtypes.float8_e5m2, 14)}[fmt]
    v = np.moveaxis(np.asarray(x, np.float32).astype(ml_dtypes.bfloat16).astype(np.float64), axis, -1)
    blocks = v.reshape(v.shape[:-1] + (-1, 32))
    amax = np.abs(blocks).max(-1, keepdims=True)
    byte = np.maximum(np.where(amax > 0, np.frexp(amax)[1] - 1 + 127, 0) - down, 1)
    scale = np.exp2(byte - 127.0)
    codes = (blocks / scale).astype(np.float32).astype(dtype).astype(np.float64)
    return np.moveaxis((codes * scale).reshape(v.shape), -1, axis)


WIDE = False


def mx_kscale(k):
    if not WIDE:
        return np.ones(k)
    levels = np.array([10, -10, 5, -5, 0])
    if k % 512:
        return np.exp2(np.random.permutation(np.resize(levels, k // 32))).repeat(32)
    a = np.empty((k // 512, 16))
    for p in range(k // 512):
        a[p, :8] = np.random.permutation(np.resize(levels, 8))
        for g in range(8):
            far = levels[np.abs(levels - a[p, g]) >= 10]
            a[p, g + 8] = far[np.random.randint(len(far))]
    return np.exp2(a.ravel()).repeat(32)


def f64(x):
    return np.asarray(x).astype(np.float64)


def striped(idx):
    return np.tile(np.asarray(idx).reshape(-1, 16).T, (8, 1)).astype(np.uint16)


def unstriped(offs):
    return offs[:16].T.reshape(-1).astype(np.int64)


E2M1 = np.array([0.0, 0.5, 1.0, 1.5, 2.0, 3.0, 4.0, 6.0, -0.0, -0.5, -1.0, -1.5, -2.0, -3.0, -4.0, -6.0])


def pack_weight(w, fmt):
    k, n = w.shape
    w = f64(np.asarray(w, np.float32).astype(ml_dtypes.bfloat16)).reshape(k // 32, 32, n)
    amax = np.abs(w).max(1)
    if fmt == "e4m3":
        byte = np.frexp(amax)[1] - 1 + 127 - 7
    else:
        mant, ex = np.frexp(amax / 6.0)
        byte = np.where(mant > 0.5, ex, ex - 1) + 127
    byte = np.clip(np.where(amax > 0, byte, 1), 1, 254)
    scaled = (w * np.exp2(127.0 - byte)[:, None, :]).reshape(k, n).astype(np.float32)
    by_word = np.ascontiguousarray(scaled.reshape(k // 512, 128, 4, n).transpose(0, 1, 3, 2))
    if fmt == "e4m3":
        words = by_word.astype(ml_dtypes.float8_e4m3fn).view(np.uint8)
    else:
        c = by_word.astype(ml_dtypes.float4_e2m1fn).view(np.uint8) & 0xF
        words = (c[..., 0::2] | (c[..., 1::2] << 4)).reshape(k // 512, 128, 2 * n)
    return np.ascontiguousarray(words), np.ascontiguousarray(byte.astype(np.uint8).reshape(k // 512, 16, n))


def unpack_weight(words, scales, fmt):
    g, _, n = scales.shape
    words = np.ascontiguousarray(words).reshape(g, 128, n, -1)
    if fmt == "e4m3":
        vals = words.view(ml_dtypes.float8_e4m3fn).astype(np.float64)
    else:
        nib = np.empty((g, 128, n, 4), np.uint8)
        nib[..., 0::2] = words & 0xF
        nib[..., 1::2] = words >> 4
        vals = E2M1[nib]
    vals = vals * np.repeat(np.exp2(scales.astype(np.float64) - 127.0), 8, axis=1)[..., None]
    return vals.transpose(0, 1, 3, 2).reshape(g * 512, n)


def bf(x):
    return np.asarray(x, np.float32).astype(ml_dtypes.bfloat16)


def planes(Y):
    r, m = Y.shape
    b = f64(bf(Y)).reshape(r // 32, 32, m)
    amax = np.abs(b).max(1)
    byte = np.clip(np.where(amax > 0, np.frexp(amax)[1] - 1 + 127 - 7, 1), 1, 254)
    codes = (b * np.exp2(127.0 - byte)[:, None, :]).reshape(r, m).astype(np.float32).astype(ml_dtypes.float8_e4m3fn).view(np.uint8)
    words = codes.reshape(r // 512, 128, 4, m).transpose(0, 1, 3, 2)
    return np.ascontiguousarray(words), np.ascontiguousarray(byte.astype(np.uint8).reshape(r // 512, 16, m))


D, T, I, Q, E, U = 512, 2048, 512, 256, 512, 512


def setup_inputs():
    n = np.random.standard_normal
    idx = np.random.permutation(T)[:I]
    idx2 = np.random.randint(0, U, I)
    fd = mx_kscale(D)
    fi = mx_kscale(I)
    ti = np.ones(T)
    ti[idx] = fi
    keysp = pack_weight(n((D, T)) / fd[:, None], "e2m1")
    return {
        "query": (n((D, Q)) * 0.4 / np.sqrt(D) * fd[:, None]).astype(np.float32),
        "keys_words": keysp[0],
        "keys_scales": keysp[1],
        "bias": (0.5 * n((Q, U))).astype(np.float32),
        "size": (np.random.uniform(0.5, 2.0, (1, I)) * fi).astype(np.float32),
        "vals": (n((E, T)) / ti).astype(np.float32),
        "offs": striped(idx),
        "offs2": striped(idx2),
    }


def reference(query, keys_words, keys_scales, bias, size, vals, offs, offs2):
    idx = unstriped(offs)
    idx2 = unstriped(offs2)
    keysu = unpack_weight(keys_words, keys_scales, "e2m1")
    queryq = mxq(f64(query), 0, "e4m3")
    keysidxg = keysu[:, idx]
    a = queryq.T @ keysidxg
    s = a + f64(bias)[:, idx2]
    p = np.exp(s - np.max(s, axis=1, keepdims=True))
    w = p * f64(size) / np.sum(p, axis=1, keepdims=True)
    wt = w.T
    vt = f64(vals)[:, idx].T
    vtq = mxq(vt, 0, "e4m3")
    wtq = mxq(wt, 0, "e4m3")
    o = vtq.T @ wtq
    words, scales = planes(o)
    return o, words, scales

@@ -1,0 +1,197 @@
+from contextlib import ExitStack
+
+import concourse.mybir as mybir
+from concourse.masks import make_identity
+
+D, T, I, Q, E, U = 512, 2048, 512, 256, 512, 512
+FLOPS = 2 * D * Q * I + 2 * I * E * Q
+
+F32 = mybir.dt.float32
+BF16 = mybir.dt.bfloat16
+I32 = mybir.dt.int32
+U32 = mybir.dt.uint32
+U16 = mybir.dt.uint16
+U8 = mybir.dt.uint8
+FP8X4 = mybir.dt.float8_e4m3fn_x4
+FP4X4 = mybir.dt.float4_e2m1fn_x4
+ALU = mybir.AluOpType
+ACT = mybir.ActivationFunctionType
+AX = mybir.AxisListType
+
+P = 128
+PACK = 4
+HALVES = Q // P
+BIAS_WINDOW = 704
+
+
+def tile_attend_bucketbias_pl_kernel(tc, query, keys_words, keys_scales, bias, size, vals, offs, offs2, out_0, out_1, out_2):
+    nc = tc.nc
+    with ExitStack() as ctx:
+        sb = ctx.enter_context(tc.tile_pool(name="sb", bufs=1))
+        ps = ctx.enter_context(tc.psum_pool(name="ps", bufs=1))
+        turn = ctx.enter_context(tc.psum_pool(name="turn", bufs=3))
+
+        slot_tok = sb.tile([P, I // 16], U16, name="slot_tok")
+        slot_bkt = sb.tile([P, I // 16], U16, name="slot_bkt")
+        key_words = sb.tile([P, T], U16, name="key_words", align_bytes=64)
+        key_scales = sb.tile([P, T], U8, name="key_scales", align_bytes=64)
+        q_raw = sb.tile([P, PACK, Q], F32, name="q_raw")
+        bias_sb = sb.tile([P, U + BIAS_WINDOW], F32, name="bias_sb")
+        size_col = sb.tile([P, PACK], F32, name="size_col")
+        val_planes = [sb.tile([P, T], F32, name=f"val_plane{r}", tag=f"plane{r}", align_bytes=64) for r in range(1, PACK)]
+        val_chunks = [sb.tile([P, T // 2], F32, name=f"val_chunk{c}") for c in range(2)]
+        ident = sb.tile([P, P], F32, name="ident")
+
+        nc.gpsimd.memset(key_scales[:].bitcast(I32), 0)
+        nc.gpsimd.memset(bias_sb[:, HALVES * U :], 0.0)
+        make_identity(nc, ident[:])
+
+        nc.sync.dma_start(slot_tok[:], offs)
+        nc.sync.dma_start(key_words[:].bitcast(I32), keys_words[0].bitcast(I32))
+        for quad in range(4):
+            nc.sync.dma_start(
+                key_scales[32 * quad : 32 * quad + 4, :].bitcast(I32),
+                keys_scales[0][4 * quad : 4 * quad + 4, :].bitcast(I32),
+            )
+        nc.sync.dma_start(q_raw[:], query.rearrange("(p t) q -> p t q", t=PACK))
+        nc.sync.dma_start(
+            bias_sb[:, : HALVES * U].rearrange("p (h u) -> p h u", h=HALVES),
+            bias.rearrange("(h p) u -> p h u", h=HALVES),
+        )
+        nc.sync.dma_start(slot_bkt[:], offs2)
+        vals_dealt = vals.rearrange("(p r) t -> p r t", r=PACK)
+        for c in range(2):
+            nc.sync.dma_start(val_chunks[c][:], vals_dealt[:, 0, c * (T // 2) : (c + 1) * (T // 2)])
+        nc.sync.dma_start(size_col[:], size.rearrange("o (p t) -> (o p) t", t=PACK))
+        for r in range(1, PACK):
+            nc.sync.dma_start(val_planes[r - 1][:], vals_dealt[:, r, :])
+
+        size_rows = ps.tile([P, PACK, P], F32, name="size_rows")
+        for t in range(PACK):
+            nc.tensor.transpose(size_rows[:, t, :], size_col[:, t : t + 1].to_broadcast([P, P]), ident[:])
+
+        kg_words = sb.tile([P, I], U16, name="kg_words", align_bytes=64)
+        kg_scales = sb.tile([P, I], U8, name="kg_scales", align_bytes=64)
+        nc.vector.tensor_copy(kg_words[:], key_words[:].indirect(slot_tok[:]))
+        nc.vector.tensor_copy(kg_scales[:], key_scales[:].indirect(slot_tok[:]))
+
+        q_bf = sb.tile([P, Q, PACK], BF16, name="q_bf", tag="q_bf", align_bytes=64)
+        nc.scalar.activation(
+            q_bf[:].rearrange("p (c i) t -> p c t i", i=4),
+            q_raw[:].rearrange("p t (c i) -> p c t i", i=4),
+            ACT.Copy,
+        )
+        q_codes = sb.tile([P, Q], U32, name="q_codes", align_bytes=64)
+        q_scales = sb.tile([P, Q], U8, name="q_scales", align_bytes=64)
+        nc.vector.quantize_mx(out=q_codes[:].bitcast(FP8X4), scales=q_scales[:], in_=q_bf[:].rearrange("p q t -> p (q t)"))
+
+        scores = [ps.tile([P, I], F32, name=f"scores{h}") for h in range(HALVES)]
+        for h in range(HALVES):
+            nc.tensor.matmul_mx(
+                out=scores[h][:],
+                lhsT=q_codes[:, h * P : (h + 1) * P].bitcast(FP8X4),
+                lhsT_scale=q_scales[:, h * P : (h + 1) * P],
+                rhs=kg_words[:].bitcast(FP4X4),
+                rhs_scale=kg_scales[:],
+                start=True,
+                stop=True,
+            )
+
+        bias_g = [
+            sb.tile([P, I], F32, name="bias_g0", align_bytes=64),
+            sb.tile([P, I], F32, name="bias_g1", tag="q_bf", align_bytes=64),
+        ]
+        for h in range(HALVES):
+            nc.vector.tensor_copy(bias_g[h][:], bias_sb[:, h * U : h * U + BIAS_WINDOW].indirect(slot_bkt[:]))
+
+        def turn_words(src_bf, dst_bf):
+            words = src_bf.bitcast(F32)
+            bank = turn.tile([P, 2, P], F32, name="turn_bank")
+            for u in range(2):
+                nc.tensor.transpose(bank[:, u, :], words[:, u::2], ident[:])
+            nc.scalar.copy(dst_bf.bitcast(F32).rearrange("p (c u) -> p c u", u=2), bank[:].rearrange("p u c -> p c u"))
+
+        vg_bf = [sb.tile([P, I], BF16, name=f"vg_bf{r}", align_bytes=64) for r in range(PACK)]
+        vt_bf = [sb.tile([P, P * PACK], BF16, name=f"vt_bf{r}", align_bytes=64) for r in range(PACK)]
+        plane0_bf = sb.tile([P, T], BF16, name="plane0_bf", tag="plane0_bf", align_bytes=64)
+        for c in range(2):
+            nc.scalar.activation(plane0_bf[:, c * (T // 2) : (c + 1) * (T // 2)], val_chunks[c][:], ACT.Copy)
+        nc.scalar.activation(vg_bf[0][:], plane0_bf[:].indirect(slot_tok[:]), ACT.Copy)
+
+        logits = [sb.tile([P, I], F32, name=f"logits{h}") for h in range(HALVES)]
+        probs_all = sb.tile([P, HALVES, I], F32, name="probs_all", tag="plane0_bf", align_bytes=64)
+        probs = [probs_all[:, h, :] for h in range(HALVES)]
+        neg_max = [sb.tile([P, 1], F32, name=f"neg_max{h}") for h in range(HALVES)]
+        row_sum = sb.tile([P, HALVES], F32, name="row_sum")
+        w_bf = [sb.tile([P, I], BF16, name=f"w_bf{h}", align_bytes=64) for h in range(HALVES)]
+        wt_bf = sb.tile([P, Q * PACK], BF16, name="wt_bf", align_bytes=64)
+        for h in range(HALVES):
+            nc.vector.tensor_tensor(logits[h][:], scores[h][:], bias_g[h][:], ALU.add)
+        for h in range(HALVES):
+            nc.vector.tensor_reduce(neg_max[h][:], logits[h][:], AX.X, ALU.max, negate=True)
+            nc.scalar.activation(probs[h], logits[h][:], ACT.Exp, bias=neg_max[h][:], accum_out=row_sum[:, h : h + 1])
+        turn_words(vg_bf[0][:], vt_bf[0][:])
+
+        def gather_plane(r):
+            nc.vector.tensor_copy(vg_bf[r][:], val_planes[r - 1][:].indirect(slot_tok[:]))
+            turn_words(vg_bf[r][:], vt_bf[r][:])
+
+        gather_plane(1)
+        inv_sum = sb.tile([P, HALVES], F32, name="inv_sum", tag="plane1", align_bytes=64)
+        nc.vector.reciprocal(inv_sum[:], row_sum[:])
+        for h in range(HALVES):
+            nc.vector.scalar_tensor_tensor(
+                w_bf[h][:].rearrange("p (s t) -> p s t", t=PACK),
+                probs[h].rearrange("p (s t) -> p s t", t=PACK),
+                inv_sum[:, h : h + 1],
+                size_rows[:].rearrange("p t s -> p s t"),
+                ALU.mult,
+                ALU.mult,
+            )
+            turn_words(w_bf[h][:], wt_bf[:, h * P * PACK : (h + 1) * P * PACK])
+        gather_plane(2)
+        gather_plane(3)
+
+        codes = sb.tile([P, Q + PACK * P], U32, name="codes", tag="plane3", align_bytes=64)
+        w_scales = sb.tile([P, Q], U8, name="w_scales", align_bytes=64)
+        v_scales = [sb.tile([P, P], U8, name=f"v_scales{r}", align_bytes=64) for r in range(PACK)]
+        w_codes = codes[:, :Q]
+        v_codes = [codes[:, Q + r * P : Q + (r + 1) * P] for r in range(PACK)]
+        nc.vector.quantize_mx(out=w_codes.bitcast(FP8X4), scales=w_scales[:], in_=wt_bf[:])
+
+        acc = [ps.tile([P, PACK, P], F32, name=f"acc{h}") for h in range(HALVES)]
+        out_dealt = out_0.rearrange("(p r) q -> p r q", r=PACK)
+        for r in range(PACK):
+            nc.vector.quantize_mx(out=v_codes[r].bitcast(FP8X4), scales=v_scales[r][:], in_=vt_bf[r][:])
+            for h in range(HALVES):
+                nc.tensor.matmul_mx(
+                    out=acc[h][:, r, :],
+                    lhsT=v_codes[r].bitcast(FP8X4),
+                    lhsT_scale=v_scales[r][:],
+                    rhs=codes[:, h * P : (h + 1) * P].bitcast(FP8X4),
+                    rhs_scale=w_scales[:, h * P : (h + 1) * P],
+                    start=True,
+                    stop=True,
+                )
+
+        y = sb.tile([P, PACK, Q], F32, name="y")
+        nc.vector.tensor_copy(y[:, :, :P], acc[0][:])
+        nc.scalar.copy(y[:, :, P:], acc[1][:])
+        nc.sync.dma_start(out_dealt, y[:])
+        y_bf = sb.tile([P, Q, PACK], BF16, name="y_bf", align_bytes=64)
+        nc.vector.tensor_copy(
+            y_bf[:, :P, :].rearrange("p (c i) r -> p c r i", i=4),
+            y[:, :, :P].rearrange("p r (c i) -> p c r i", i=4),
+        )
+        nc.scalar.copy(y_bf[:, P:, :], acc[1][:].rearrange("p r q -> p q r"))
+        y_codes = sb.tile([P, Q], U32, name="y_codes", align_bytes=64)
+        y_scales = sb.tile([P, Q], U8, name="y_scales", align_bytes=64)
+        nc.vector.quantize_mx(out=y_codes[:].bitcast(FP8X4), scales=y_scales[:], in_=y_bf[:].rearrange("p q r -> p (q r)"))
+
+        nc.sync.dma_start(out_1[0].rearrange("p c r -> p (c r)").bitcast(I32), y_codes[:].bitcast(I32))
+        for quad in range(4):
+            queue = nc.sync if quad % 2 == 0 else nc.scalar
+            queue.dma_start(
+                out_2[0][4 * quad : 4 * quad + 4, :].bitcast(I32),
+                y_scales[32 * quad : 32 * quad + 4, :].bitcast(I32),
+            )

@@ -22,6 +22,7 @@ P = 128
 PACK = 4
 HALVES = Q // P
 BIAS_WINDOW = 704
+VECTOR_COLUMNS = 160
 
 
 def tile_attend_bucketbias_pl_kernel(tc, query, keys_words, keys_scales, bias, size, vals, offs, offs2, out_0, out_1, out_2):
@@ -36,29 +37,32 @@ def tile_attend_bucketbias_pl_kernel(tc, query, keys_words, keys_scales, bias, s
         key_words = sb.tile([P, T], U16, name="key_words", align_bytes=64)
         key_scales = sb.tile([P, T], U8, name="key_scales", align_bytes=64)
         q_raw = sb.tile([P, PACK, Q], F32, name="q_raw")
-        bias_sb = sb.tile([P, U + BIAS_WINDOW], F32, name="bias_sb")
+        bias_sb = [sb.tile([P, BIAS_WINDOW], F32, name=f"bias_sb{h}") for h in range(HALVES)]
         size_col = sb.tile([P, PACK], F32, name="size_col")
         val_planes = [sb.tile([P, T], F32, name=f"val_plane{r}", tag=f"plane{r}", align_bytes=64) for r in range(1, PACK)]
         val_chunks = [sb.tile([P, T // 2], F32, name=f"val_chunk{c}") for c in range(2)]
         ident = sb.tile([P, P], F32, name="ident")
 
         nc.gpsimd.memset(key_scales[:].bitcast(I32), 0)
-        nc.gpsimd.memset(bias_sb[:, HALVES * U :], 0.0)
-        make_identity(nc, ident[:])
+        for h in range(HALVES):
+            nc.vector.memset(bias_sb[h][:, U:], 0.0)
 
-        nc.sync.dma_start(slot_tok[:], offs)
-        nc.sync.dma_start(key_words[:].bitcast(I32), keys_words[0].bitcast(I32))
-        for quad in range(4):
-            nc.sync.dma_start(
+        def load_key_scales(queue, quad):
+            queue.dma_start(
                 key_scales[32 * quad : 32 * quad + 4, :].bitcast(I32),
                 keys_scales[0][4 * quad : 4 * quad + 4, :].bitcast(I32),
             )
-        nc.sync.dma_start(q_raw[:], query.rearrange("(p t) q -> p t q", t=PACK))
-        nc.sync.dma_start(
-            bias_sb[:, : HALVES * U].rearrange("p (h u) -> p h u", h=HALVES),
-            bias.rearrange("(h p) u -> p h u", h=HALVES),
-        )
+
+        make_identity(nc, ident[:])
+
         nc.sync.dma_start(slot_bkt[:], offs2)
+        nc.sync.dma_start(bias_sb[0][:, :U], bias[:P, :])
+        nc.sync.dma_start(slot_tok[:], offs)
+        nc.sync.dma_start(key_words[:].bitcast(I32), keys_words[0].bitcast(I32))
+        for quad in range(4):
+            load_key_scales(nc.sync, quad)
+        nc.sync.dma_start(q_raw[:], query.rearrange("(p t) q -> p t q", t=PACK))
+        nc.sync.dma_start(bias_sb[1][:, :U], bias[P:, :])
         vals_dealt = vals.rearrange("(p r) t -> p r t", r=PACK)
         for c in range(2):
             nc.sync.dma_start(val_chunks[c][:], vals_dealt[:, 0, c * (T // 2) : (c + 1) * (T // 2)])
@@ -85,7 +89,7 @@ def tile_attend_bucketbias_pl_kernel(tc, query, keys_words, keys_scales, bias, s
         q_scales = sb.tile([P, Q], U8, name="q_scales", align_bytes=64)
         nc.vector.quantize_mx(out=q_codes[:].bitcast(FP8X4), scales=q_scales[:], in_=q_bf[:].rearrange("p q t -> p (q t)"))
 
-        scores = [ps.tile([P, I], F32, name=f"scores{h}") for h in range(HALVES)]
+        scores = [ps.tile([P, I], F32, name=f"scores{h}", tag=f"bank{h}") for h in range(HALVES)]
         for h in range(HALVES):
             nc.tensor.matmul_mx(
                 out=scores[h][:],
@@ -102,7 +106,7 @@ def tile_attend_bucketbias_pl_kernel(tc, query, keys_words, keys_scales, bias, s
             sb.tile([P, I], F32, name="bias_g1", tag="q_bf", align_bytes=64),
         ]
         for h in range(HALVES):
-            nc.vector.tensor_copy(bias_g[h][:], bias_sb[:, h * U : h * U + BIAS_WINDOW].indirect(slot_bkt[:]))
+            nc.vector.tensor_copy(bias_g[h][:], bias_sb[h][:].indirect(slot_bkt[:]))
 
         def turn_words(src_bf, dst_bf):
             words = src_bf.bitcast(F32)
@@ -112,14 +116,21 @@ def tile_attend_bucketbias_pl_kernel(tc, query, keys_words, keys_scales, bias, s
             nc.scalar.copy(dst_bf.bitcast(F32).rearrange("p (c u) -> p c u", u=2), bank[:].rearrange("p u c -> p c u"))
 
         vg_bf = [sb.tile([P, I], BF16, name=f"vg_bf{r}", align_bytes=64) for r in range(PACK)]
-        vt_bf = [sb.tile([P, P * PACK], BF16, name=f"vt_bf{r}", align_bytes=64) for r in range(PACK)]
+        vt_all = sb.tile([P, PACK * I], BF16, name="vt_all", align_bytes=64)
+        vt_bf = [vt_all[:, r * I : (r + 1) * I] for r in range(PACK)]
         plane0_bf = sb.tile([P, T], BF16, name="plane0_bf", tag="plane0_bf", align_bytes=64)
         for c in range(2):
             nc.scalar.activation(plane0_bf[:, c * (T // 2) : (c + 1) * (T // 2)], val_chunks[c][:], ACT.Copy)
-        nc.scalar.activation(vg_bf[0][:], plane0_bf[:].indirect(slot_tok[:]), ACT.Copy)
+
+        def gather_plane0_half(c):
+            n = I // 2
+            offsets = slot_tok[:, c * n // 16 : (c + 1) * n // 16]
+            nc.scalar.activation(vg_bf[0][:, c * n : (c + 1) * n], plane0_bf[:].indirect(offsets), ACT.Copy)
+
+        gather_plane0_half(0)
 
         logits = [sb.tile([P, I], F32, name=f"logits{h}") for h in range(HALVES)]
-        probs_all = sb.tile([P, HALVES, I], F32, name="probs_all", tag="plane0_bf", align_bytes=64)
+        probs_all = sb.tile([P, HALVES, I], F32, name="probs_all", align_bytes=64)
         probs = [probs_all[:, h, :] for h in range(HALVES)]
         neg_max = [sb.tile([P, 1], F32, name=f"neg_max{h}") for h in range(HALVES)]
         row_sum = sb.tile([P, HALVES], F32, name="row_sum")
@@ -130,11 +141,11 @@ def tile_attend_bucketbias_pl_kernel(tc, query, keys_words, keys_scales, bias, s
         for h in range(HALVES):
             nc.vector.tensor_reduce(neg_max[h][:], logits[h][:], AX.X, ALU.max, negate=True)
             nc.scalar.activation(probs[h], logits[h][:], ACT.Exp, bias=neg_max[h][:], accum_out=row_sum[:, h : h + 1])
-        turn_words(vg_bf[0][:], vt_bf[0][:])
+        gather_plane0_half(1)
 
         def gather_plane(r):
             nc.vector.tensor_copy(vg_bf[r][:], val_planes[r - 1][:].indirect(slot_tok[:]))
-            turn_words(vg_bf[r][:], vt_bf[r][:])
+            turn_words(vg_bf[r][:], vt_bf[r])
 
         gather_plane(1)
         inv_sum = sb.tile([P, HALVES], F32, name="inv_sum", tag="plane1", align_bytes=64)
@@ -149,48 +160,59 @@ def tile_attend_bucketbias_pl_kernel(tc, query, keys_words, keys_scales, bias, s
                 ALU.mult,
             )
             turn_words(w_bf[h][:], wt_bf[:, h * P * PACK : (h + 1) * P * PACK])
+        turn_words(vg_bf[0][:], vt_bf[0])
         gather_plane(2)
         gather_plane(3)
 
         codes = sb.tile([P, Q + PACK * P], U32, name="codes", tag="plane3", align_bytes=64)
         w_scales = sb.tile([P, Q], U8, name="w_scales", align_bytes=64)
-        v_scales = [sb.tile([P, P], U8, name=f"v_scales{r}", align_bytes=64) for r in range(PACK)]
-        w_codes = codes[:, :Q]
-        v_codes = [codes[:, Q + r * P : Q + (r + 1) * P] for r in range(PACK)]
-        nc.vector.quantize_mx(out=w_codes.bitcast(FP8X4), scales=w_scales[:], in_=wt_bf[:])
-
-        acc = [ps.tile([P, PACK, P], F32, name=f"acc{h}") for h in range(HALVES)]
-        out_dealt = out_0.rearrange("(p r) q -> p r q", r=PACK)
+        v_scales = sb.tile([P, PACK * P], U8, name="v_scales", align_bytes=64)
+        nc.vector.quantize_mx(out=codes[:, :Q].bitcast(FP8X4), scales=w_scales[:], in_=wt_bf[:])
         for r in range(PACK):
-            nc.vector.quantize_mx(out=v_codes[r].bitcast(FP8X4), scales=v_scales[r][:], in_=vt_bf[r][:])
-            for h in range(HALVES):
-                nc.tensor.matmul_mx(
-                    out=acc[h][:, r, :],
-                    lhsT=v_codes[r].bitcast(FP8X4),
-                    lhsT_scale=v_scales[r][:],
-                    rhs=codes[:, h * P : (h + 1) * P].bitcast(FP8X4),
-                    rhs_scale=w_scales[:, h * P : (h + 1) * P],
-                    start=True,
-                    stop=True,
-                )
+            nc.vector.quantize_mx(
+                out=codes[:, Q + r * P : Q + (r + 1) * P].bitcast(FP8X4),
+                scales=v_scales[:, r * P : (r + 1) * P],
+                in_=vt_bf[r],
+            )
 
-        y = sb.tile([P, PACK, Q], F32, name="y")
-        nc.vector.tensor_copy(y[:, :, :P], acc[0][:])
-        nc.scalar.copy(y[:, :, P:], acc[1][:])
-        nc.sync.dma_start(out_dealt, y[:])
+        out_dealt = out_0.rearrange("(p r) q -> p r q", r=PACK)
+        last = PACK - 1
+        y = sb.tile([P, PACK * Q], F32, name="y")
+        for r in range(PACK):
+            acc = ps.tile([P, Q], F32, name=f"acc{r}", tag=f"bank{r}")
+            nc.tensor.matmul_mx(
+                out=acc[:],
+                lhsT=codes[:, Q + r * P : Q + (r + 1) * P].bitcast(FP8X4),
+                lhsT_scale=v_scales[:, r * P : (r + 1) * P],
+                rhs=codes[:, :Q].bitcast(FP8X4),
+                rhs_scale=w_scales[:],
+                start=True,
+                stop=True,
+            )
+            if r < last:
+                nc.scalar.copy(y[:, r * Q : (r + 1) * Q], acc[:])
+            else:
+                nc.vector.tensor_copy(y[:, r * Q : (r + 1) * Q], acc[:])
+        nc.sync.dma_start(out_dealt[:, :last, :], y[:, : last * Q].rearrange("p (r q) -> p r q", r=last))
+        nc.sync.dma_start(out_dealt[:, last, :], y[:, last * Q :])
+
         y_bf = sb.tile([P, Q, PACK], BF16, name="y_bf", align_bytes=64)
+        y_planes = y[:].rearrange("p (r q) -> p r q", r=PACK)
         nc.vector.tensor_copy(
-            y_bf[:, :P, :].rearrange("p (c i) r -> p c r i", i=4),
-            y[:, :, :P].rearrange("p r (c i) -> p c r i", i=4),
+            y_bf[:, :VECTOR_COLUMNS, :].rearrange("p (c i) r -> p c r i", i=4),
+            y_planes[:, :, :VECTOR_COLUMNS].rearrange("p r (c i) -> p c r i", i=4),
         )
-        nc.scalar.copy(y_bf[:, P:, :], acc[1][:].rearrange("p r q -> p q r"))
+        nc.scalar.copy(
+            y_bf[:, VECTOR_COLUMNS:, :].rearrange("p (c i) r -> p c r i", i=4),
+            y_planes[:, :, VECTOR_COLUMNS:].rearrange("p r (c i) -> p c r i", i=4),
+        )
         y_codes = sb.tile([P, Q], U32, name="y_codes", align_bytes=64)
         y_scales = sb.tile([P, Q], U8, name="y_scales", align_bytes=64)
         nc.vector.quantize_mx(out=y_codes[:].bitcast(FP8X4), scales=y_scales[:], in_=y_bf[:].rearrange("p q r -> p (q r)"))
 
         nc.sync.dma_start(out_1[0].rearrange("p c r -> p (c r)").bitcast(I32), y_codes[:].bitcast(I32))
         for quad in range(4):
-            queue = nc.sync if quad % 2 == 0 else nc.scalar
+            queue = nc.scalar if quad % 2 == 0 else nc.sync
             queue.dma_start(
                 out_2[0][4 * quad : 4 * quad + 4, :].bitcast(I32),
                 y_scales[32 * quad : 32 * quad + 4, :].bitcast(I32),

@@ -22,7 +22,7 @@ P = 128
 PACK = 4
 HALVES = Q // P
 BIAS_WINDOW = 704
-VECTOR_COLUMNS = 160
+VECTOR_COLUMNS = 176
 
 
 def tile_attend_bucketbias_pl_kernel(tc, query, keys_words, keys_scales, bias, size, vals, offs, offs2, out_0, out_1, out_2):
@@ -189,7 +189,7 @@ def tile_attend_bucketbias_pl_kernel(tc, query, keys_words, keys_scales, bias, s
                 start=True,
                 stop=True,
             )
-            if r < last:
+            if r != last - 1:
                 nc.scalar.copy(y[:, r * Q : (r + 1) * Q], acc[:])
             else:
                 nc.vector.tensor_copy(y[:, r * Q : (r + 1) * Q], acc[:])

@@ -22,7 +22,6 @@ P = 128
 PACK = 4
 HALVES = Q // P
 BIAS_WINDOW = 704
-VECTOR_COLUMNS = 176
 
 
 def tile_attend_bucketbias_pl_kernel(tc, query, keys_words, keys_scales, bias, size, vals, offs, offs2, out_0, out_1, out_2):
@@ -70,9 +69,10 @@ def tile_attend_bucketbias_pl_kernel(tc, query, keys_words, keys_scales, bias, s
         for r in range(1, PACK):
             nc.sync.dma_start(val_planes[r - 1][:], vals_dealt[:, r, :])
 
-        size_rows = ps.tile([P, PACK, P], F32, name="size_rows")
+        size_rows = ps.tile([P, I], F32, name="size_rows")
+        size_places = size_rows[:].rearrange("p (u g x t) -> p t g u x", u=2, x=4, t=PACK)
         for t in range(PACK):
-            nc.tensor.transpose(size_rows[:, t, :], size_col[:, t : t + 1].to_broadcast([P, P]), ident[:])
+            nc.tensor.transpose(size_places[:, t], size_col[:, t : t + 1].to_broadcast([P, P]), ident[:])
 
         kg_words = sb.tile([P, I], U16, name="kg_words", align_bytes=64)
         kg_scales = sb.tile([P, I], U8, name="kg_scales", align_bytes=64)
@@ -108,16 +108,21 @@ def tile_attend_bucketbias_pl_kernel(tc, query, keys_words, keys_scales, bias, s
         for h in range(HALVES):
             nc.vector.tensor_copy(bias_g[h][:], bias_sb[h][:].indirect(slot_bkt[:]))
 
+        def dealt(ap):
+            return ap.rearrange("p (u g x) -> p g u x", u=2, x=16)
+
         def turn_words(src_bf, dst_bf):
             words = src_bf.bitcast(F32)
             bank = turn.tile([P, 2, P], F32, name="turn_bank")
             for u in range(2):
-                nc.tensor.transpose(bank[:, u, :], words[:, u::2], ident[:])
+                nc.tensor.transpose(bank[:, u, :], words[:, u * P : (u + 1) * P], ident[:])
             nc.scalar.copy(dst_bf.bitcast(F32).rearrange("p (c u) -> p c u", u=2), bank[:].rearrange("p u c -> p c u"))
 
-        vg_bf = [sb.tile([P, I], BF16, name=f"vg_bf{r}", align_bytes=64) for r in range(PACK)]
-        vt_all = sb.tile([P, PACK * I], BF16, name="vt_all", align_bytes=64)
-        vt_bf = [vt_all[:, r * I : (r + 1) * I] for r in range(PACK)]
+        vg_bf = [sb.tile([P, I], BF16, name=f"vg_bf{r}", align_bytes=64) for r in range(PACK - 1)]
+        early_bf = sb.tile([P, Q * PACK + 2 * I], BF16, name="early_bf", tag="early_bf", align_bytes=64)
+        late_bf = sb.tile([P, 2 * I], BF16, name="late_bf", align_bytes=64)
+        wt_bf = early_bf[:, : Q * PACK]
+        vt_bf = [early_bf[:, Q * PACK : Q * PACK + I], early_bf[:, Q * PACK + I :], late_bf[:, :I], late_bf[:, I:]]
         plane0_bf = sb.tile([P, T], BF16, name="plane0_bf", tag="plane0_bf", align_bytes=64)
         for c in range(2):
             nc.scalar.activation(plane0_bf[:, c * (T // 2) : (c + 1) * (T // 2)], val_chunks[c][:], ACT.Copy)
@@ -125,7 +130,7 @@ def tile_attend_bucketbias_pl_kernel(tc, query, keys_words, keys_scales, bias, s
         def gather_plane0_half(c):
             n = I // 2
             offsets = slot_tok[:, c * n // 16 : (c + 1) * n // 16]
-            nc.scalar.activation(vg_bf[0][:, c * n : (c + 1) * n], plane0_bf[:].indirect(offsets), ACT.Copy)
+            nc.scalar.activation(dealt(vg_bf[0][:])[:, c * 8 : (c + 1) * 8], plane0_bf[:].indirect(offsets), ACT.Copy)
 
         gather_plane0_half(0)
 
@@ -135,77 +140,83 @@ def tile_attend_bucketbias_pl_kernel(tc, query, keys_words, keys_scales, bias, s
         neg_max = [sb.tile([P, 1], F32, name=f"neg_max{h}") for h in range(HALVES)]
         row_sum = sb.tile([P, HALVES], F32, name="row_sum")
         w_bf = [sb.tile([P, I], BF16, name=f"w_bf{h}", align_bytes=64) for h in range(HALVES)]
-        wt_bf = sb.tile([P, Q * PACK], BF16, name="wt_bf", align_bytes=64)
         for h in range(HALVES):
-            nc.vector.tensor_tensor(logits[h][:], scores[h][:], bias_g[h][:], ALU.add)
+            nc.vector.tensor_tensor(
+                logits[h][:].rearrange("p (u g x) -> p u g x", u=2, x=16),
+                scores[h][:].rearrange("p (g u x) -> p u g x", u=2, x=16),
+                bias_g[h][:].rearrange("p (g u x) -> p u g x", u=2, x=16),
+                ALU.add,
+            )
         for h in range(HALVES):
             nc.vector.tensor_reduce(neg_max[h][:], logits[h][:], AX.X, ALU.max, negate=True)
             nc.scalar.activation(probs[h], logits[h][:], ACT.Exp, bias=neg_max[h][:], accum_out=row_sum[:, h : h + 1])
         gather_plane0_half(1)
 
         def gather_plane(r):
-            nc.vector.tensor_copy(vg_bf[r][:], val_planes[r - 1][:].indirect(slot_tok[:]))
+            nc.vector.tensor_copy(dealt(vg_bf[r][:]), val_planes[r - 1][:].indirect(slot_tok[:]))
             turn_words(vg_bf[r][:], vt_bf[r])
 
         gather_plane(1)
+        turn_words(vg_bf[0][:], vt_bf[0])
         inv_sum = sb.tile([P, HALVES], F32, name="inv_sum", tag="plane1", align_bytes=64)
         nc.vector.reciprocal(inv_sum[:], row_sum[:])
         for h in range(HALVES):
             nc.vector.scalar_tensor_tensor(
-                w_bf[h][:].rearrange("p (s t) -> p s t", t=PACK),
-                probs[h].rearrange("p (s t) -> p s t", t=PACK),
+                w_bf[h][:],
+                probs[h],
                 inv_sum[:, h : h + 1],
-                size_rows[:].rearrange("p t s -> p s t"),
+                size_rows[:],
                 ALU.mult,
                 ALU.mult,
             )
             turn_words(w_bf[h][:], wt_bf[:, h * P * PACK : (h + 1) * P * PACK])
-        turn_words(vg_bf[0][:], vt_bf[0])
         gather_plane(2)
-        gather_plane(3)
 
-        codes = sb.tile([P, Q + PACK * P], U32, name="codes", tag="plane3", align_bytes=64)
-        w_scales = sb.tile([P, Q], U8, name="w_scales", align_bytes=64)
-        v_scales = sb.tile([P, PACK * P], U8, name="v_scales", align_bytes=64)
-        nc.vector.quantize_mx(out=codes[:, :Q].bitcast(FP8X4), scales=w_scales[:], in_=wt_bf[:])
-        for r in range(PACK):
-            nc.vector.quantize_mx(
-                out=codes[:, Q + r * P : Q + (r + 1) * P].bitcast(FP8X4),
-                scales=v_scales[:, r * P : (r + 1) * P],
-                in_=vt_bf[r],
-            )
+        early_codes = sb.tile([P, Q + 2 * P], U32, name="early_codes", tag="plane2", align_bytes=64)
+        late_codes = sb.tile([P, 2 * P], U32, name="late_codes", tag="plane3", align_bytes=64)
+        all_scales = sb.tile([P, Q + PACK * P], U8, name="all_scales", align_bytes=64)
+        w_scales = all_scales[:, :Q]
+        v_scales = all_scales[:, Q:]
+        w_codes = early_codes[:, :Q]
+        v_codes = [early_codes[:, Q : Q + P], early_codes[:, Q + P :], late_codes[:, :P], late_codes[:, P:]]
+        nc.vector.quantize_mx(out=early_codes[:].bitcast(FP8X4), scales=all_scales[:, : Q + 2 * P], in_=early_bf[:])
 
         out_dealt = out_0.rearrange("(p r) q -> p r q", r=PACK)
-        last = PACK - 1
-        y = sb.tile([P, PACK * Q], F32, name="y")
-        for r in range(PACK):
-            acc = ps.tile([P, Q], F32, name=f"acc{r}", tag=f"bank{r}")
-            nc.tensor.matmul_mx(
-                out=acc[:],
-                lhsT=codes[:, Q + r * P : Q + (r + 1) * P].bitcast(FP8X4),
-                lhsT_scale=v_scales[:, r * P : (r + 1) * P],
-                rhs=codes[:, :Q].bitcast(FP8X4),
-                rhs_scale=w_scales[:],
-                start=True,
-                stop=True,
-            )
-            if r != last - 1:
-                nc.scalar.copy(y[:, r * Q : (r + 1) * Q], acc[:])
-            else:
-                nc.vector.tensor_copy(y[:, r * Q : (r + 1) * Q], acc[:])
-        nc.sync.dma_start(out_dealt[:, :last, :], y[:, : last * Q].rearrange("p (r q) -> p r q", r=last))
-        nc.sync.dma_start(out_dealt[:, last, :], y[:, last * Q :])
+        y = sb.tile([P, PACK, Q], F32, name="y")
+        acc = [ps.tile([P, PACK, P], F32, name=f"acc{h}", tag=f"bank{h}") for h in range(HALVES)]
+
+        def multiply(r):
+            for h in range(HALVES):
+                nc.tensor.matmul_mx(
+                    out=acc[h][:, r, :],
+                    lhsT=v_codes[r].bitcast(FP8X4),
+                    lhsT_scale=v_scales[:, r * P : (r + 1) * P],
+                    rhs=w_codes[:, h * P : (h + 1) * P].bitcast(FP8X4),
+                    rhs_scale=w_scales[:, h * P : (h + 1) * P],
+                    start=True,
+                    stop=True,
+                )
+
+        def store_planes(first, end, copy_first_half=nc.scalar.copy):
+            copy_first_half(y[:, first:end, :P], acc[0][:, first:end, :])
+            nc.scalar.copy(y[:, first:end, P:], acc[1][:, first:end, :])
+            nc.sync.dma_start(out_dealt[:, first:end, :], y[:, first:end, :])
+
+        multiply(0)
+        multiply(1)
+        store_planes(0, 2)
+        vg_bf.append(sb.tile([P, I], BF16, name="vg_bf3", align_bytes=64))
+        gather_plane(3)
+        nc.vector.quantize_mx(out=v_codes[2].bitcast(FP8X4), scales=v_scales[:, 2 * P : 3 * P], in_=vt_bf[2])
+        multiply(2)
+        store_planes(2, 3, nc.vector.tensor_copy)
+        nc.vector.quantize_mx(out=v_codes[3].bitcast(FP8X4), scales=v_scales[:, 3 * P :], in_=vt_bf[3])
+        multiply(3)
 
         y_bf = sb.tile([P, Q, PACK], BF16, name="y_bf", align_bytes=64)
-        y_planes = y[:].rearrange("p (r q) -> p r q", r=PACK)
-        nc.vector.tensor_copy(
-            y_bf[:, :VECTOR_COLUMNS, :].rearrange("p (c i) r -> p c r i", i=4),
-            y_planes[:, :, :VECTOR_COLUMNS].rearrange("p r (c i) -> p c r i", i=4),
-        )
-        nc.scalar.copy(
-            y_bf[:, VECTOR_COLUMNS:, :].rearrange("p (c i) r -> p c r i", i=4),
-            y_planes[:, :, VECTOR_COLUMNS:].rearrange("p r (c i) -> p c r i", i=4),
-        )
+        nc.vector.tensor_copy(y_bf[:, :P, :], acc[0][:].rearrange("p r q -> p q r"))
+        nc.scalar.copy(y_bf[:, P:, :], acc[1][:].rearrange("p r q -> p q r"))
+        store_planes(3, PACK)
         y_codes = sb.tile([P, Q], U32, name="y_codes", align_bytes=64)
         y_scales = sb.tile([P, Q], U8, name="y_scales", align_bytes=64)
         nc.vector.quantize_mx(out=y_codes[:].bitcast(FP8X4), scales=y_scales[:], in_=y_bf[:].rearrange("p q r -> p (q r)"))

@@ -35,7 +35,7 @@ def tile_attend_bucketbias_pl_kernel(tc, query, keys_words, keys_scales, bias, s
         slot_bkt = sb.tile([P, I // 16], U16, name="slot_bkt")
         key_words = sb.tile([P, T], U16, name="key_words", align_bytes=64)
         key_scales = sb.tile([P, T], U8, name="key_scales", align_bytes=64)
-        q_raw = sb.tile([P, PACK, Q], F32, name="q_raw")
+        q_raw = sb.tile([P, PACK, Q], F32, name="q_raw", tag="q_raw", align_bytes=64)
         bias_sb = [sb.tile([P, BIAS_WINDOW], F32, name=f"bias_sb{h}") for h in range(HALVES)]
         size_col = sb.tile([P, PACK], F32, name="size_col")
         val_planes = [sb.tile([P, T], F32, name=f"val_plane{r}", tag=f"plane{r}", align_bytes=64) for r in range(1, PACK)]
@@ -46,25 +46,20 @@ def tile_attend_bucketbias_pl_kernel(tc, query, keys_words, keys_scales, bias, s
         for h in range(HALVES):
             nc.vector.memset(bias_sb[h][:, U:], 0.0)
 
-        def load_key_scales(queue, quad):
-            queue.dma_start(
-                key_scales[32 * quad : 32 * quad + 4, :].bitcast(I32),
-                keys_scales[0][4 * quad : 4 * quad + 4, :].bitcast(I32),
-            )
-
         make_identity(nc, ident[:])
 
         nc.sync.dma_start(slot_bkt[:], offs2)
         nc.sync.dma_start(bias_sb[0][:, :U], bias[:P, :])
         nc.sync.dma_start(slot_tok[:], offs)
         nc.sync.dma_start(key_words[:].bitcast(I32), keys_words[0].bitcast(I32))
-        for quad in range(4):
-            load_key_scales(nc.sync, quad)
+        for row in range(4):
+            nc.sync.dma_start(key_scales[row:P:32, :].bitcast(I32), keys_scales[0][row:16:4, :].bitcast(I32))
         nc.sync.dma_start(q_raw[:], query.rearrange("(p t) q -> p t q", t=PACK))
-        nc.sync.dma_start(bias_sb[1][:, :U], bias[P:, :])
         vals_dealt = vals.rearrange("(p r) t -> p r t", r=PACK)
         for c in range(2):
             nc.sync.dma_start(val_chunks[c][:], vals_dealt[:, 0, c * (T // 2) : (c + 1) * (T // 2)])
+            if c == 0:
+                nc.sync.dma_start(bias_sb[1][:, :U], bias[P:, :])
         nc.sync.dma_start(size_col[:], size.rearrange("o (p t) -> (o p) t", t=PACK))
         for r in range(1, PACK):
             nc.sync.dma_start(val_planes[r - 1][:], vals_dealt[:, r, :])
@@ -103,7 +98,7 @@ def tile_attend_bucketbias_pl_kernel(tc, query, keys_words, keys_scales, bias, s
 
         bias_g = [
             sb.tile([P, I], F32, name="bias_g0", align_bytes=64),
-            sb.tile([P, I], F32, name="bias_g1", tag="q_bf", align_bytes=64),
+            sb.tile([P, I], F32, name="bias_g1", tag="q_raw", align_bytes=64),
         ]
         for h in range(HALVES):
             nc.vector.tensor_copy(bias_g[h][:], bias_sb[h][:].indirect(slot_bkt[:]))
@@ -197,9 +192,9 @@ def tile_attend_bucketbias_pl_kernel(tc, query, keys_words, keys_scales, bias, s
                     stop=True,
                 )
 
-        def store_planes(first, end, copy_first_half=nc.scalar.copy):
-            copy_first_half(y[:, first:end, :P], acc[0][:, first:end, :])
-            nc.scalar.copy(y[:, first:end, P:], acc[1][:, first:end, :])
+        def store_planes(first, end):
+            for h in range(HALVES):
+                nc.scalar.copy(y[:, first:end, h * P : (h + 1) * P], acc[h][:, first:end, :])
             nc.sync.dma_start(out_dealt[:, first:end, :], y[:, first:end, :])
 
         multiply(0)
@@ -209,7 +204,7 @@ def tile_attend_bucketbias_pl_kernel(tc, query, keys_words, keys_scales, bias, s
         gather_plane(3)
         nc.vector.quantize_mx(out=v_codes[2].bitcast(FP8X4), scales=v_scales[:, 2 * P : 3 * P], in_=vt_bf[2])
         multiply(2)
-        store_planes(2, 3, nc.vector.tensor_copy)
+        store_planes(2, 3)
         nc.vector.quantize_mx(out=v_codes[3].bitcast(FP8X4), scales=v_scales[:, 3 * P :], in_=vt_bf[3])
         multiply(3)
 

@@ -60,9 +60,10 @@ def tile_attend_bucketbias_pl_kernel(tc, query, keys_words, keys_scales, bias, s
             nc.sync.dma_start(val_chunks[c][:], vals_dealt[:, 0, c * (T // 2) : (c + 1) * (T // 2)])
             if c == 0:
                 nc.sync.dma_start(bias_sb[1][:, :U], bias[P:, :])
-        nc.sync.dma_start(size_col[:], size.rearrange("o (p t) -> (o p) t", t=PACK))
         for r in range(1, PACK):
             nc.sync.dma_start(val_planes[r - 1][:], vals_dealt[:, r, :])
+            if r == 1:
+                nc.sync.dma_start(size_col[:], size.rearrange("o (p t) -> (o p) t", t=PACK))
 
         size_rows = ps.tile([P, I], F32, name="size_rows")
         size_places = size_rows[:].rearrange("p (u g x t) -> p t g u x", u=2, x=4, t=PACK)
@@ -134,6 +135,9 @@ def tile_attend_bucketbias_pl_kernel(tc, query, keys_words, keys_scales, bias, s
         probs = [probs_all[:, h, :] for h in range(HALVES)]
         neg_max = [sb.tile([P, 1], F32, name=f"neg_max{h}") for h in range(HALVES)]
         row_sum = sb.tile([P, HALVES], F32, name="row_sum")
+        inv_sum = sb.tile([P, HALVES], F32, name="inv_sum")
+        minus_one = sb.tile([P, 1], F32, name="minus_one")
+        nc.gpsimd.memset(minus_one[:], -1.0)
         w_bf = [sb.tile([P, I], BF16, name=f"w_bf{h}", align_bytes=64) for h in range(HALVES)]
         for h in range(HALVES):
             nc.vector.tensor_tensor(
@@ -145,6 +149,7 @@ def tile_attend_bucketbias_pl_kernel(tc, query, keys_words, keys_scales, bias, s
         for h in range(HALVES):
             nc.vector.tensor_reduce(neg_max[h][:], logits[h][:], AX.X, ALU.max, negate=True)
             nc.scalar.activation(probs[h], logits[h][:], ACT.Exp, bias=neg_max[h][:], accum_out=row_sum[:, h : h + 1])
+            nc.gpsimd.tensor_tensor(inv_sum[:, h : h + 1], row_sum[:, h : h + 1], minus_one[:], ALU.pow)
         gather_plane0_half(1)
 
         def gather_plane(r):
@@ -153,8 +158,6 @@ def tile_attend_bucketbias_pl_kernel(tc, query, keys_words, keys_scales, bias, s
 
         gather_plane(1)
         turn_words(vg_bf[0][:], vt_bf[0])
-        inv_sum = sb.tile([P, HALVES], F32, name="inv_sum", tag="plane1", align_bytes=64)
-        nc.vector.reciprocal(inv_sum[:], row_sum[:])
         for h in range(HALVES):
             nc.vector.scalar_tensor_tensor(
                 w_bf[h][:],
@@ -174,7 +177,8 @@ def tile_attend_bucketbias_pl_kernel(tc, query, keys_words, keys_scales, bias, s
         v_scales = all_scales[:, Q:]
         w_codes = early_codes[:, :Q]
         v_codes = [early_codes[:, Q : Q + P], early_codes[:, Q + P :], late_codes[:, :P], late_codes[:, P:]]
-        nc.vector.quantize_mx(out=early_codes[:].bitcast(FP8X4), scales=all_scales[:, : Q + 2 * P], in_=early_bf[:])
+        nc.vector.quantize_mx(out=early_codes[:, Q:].bitcast(FP8X4), scales=v_scales[:, : 2 * P], in_=early_bf[:, Q * PACK :])
+        nc.vector.quantize_mx(out=w_codes.bitcast(FP8X4), scales=w_scales, in_=wt_bf)
 
         out_dealt = out_0.rearrange("(p r) q -> p r q", r=PACK)
         y = sb.tile([P, PACK, Q], F32, name="y")

@@ -196,29 +196,38 @@ def tile_attend_bucketbias_pl_kernel(tc, query, keys_words, keys_scales, bias, s
                     stop=True,
                 )
 
+        def leave_bank(h, first, end, copy):
+            copy(y[:, first:end, h * P : (h + 1) * P], acc[h][:, first:end, :])
+
         def store_planes(first, end):
-            for h in range(HALVES):
-                nc.scalar.copy(y[:, first:end, h * P : (h + 1) * P], acc[h][:, first:end, :])
             nc.sync.dma_start(out_dealt[:, first:end, :], y[:, first:end, :])
 
         multiply(0)
         multiply(1)
+        for h in range(HALVES):
+            leave_bank(h, 0, 2, nc.scalar.copy)
         store_planes(0, 2)
         vg_bf.append(sb.tile([P, I], BF16, name="vg_bf3", align_bytes=64))
         gather_plane(3)
         nc.vector.quantize_mx(out=v_codes[2].bitcast(FP8X4), scales=v_scales[:, 2 * P : 3 * P], in_=vt_bf[2])
         multiply(2)
+        leave_bank(0, 2, 3, nc.vector.tensor_copy)
+        leave_bank(1, 2, 3, nc.scalar.copy)
         store_planes(2, 3)
         nc.vector.quantize_mx(out=v_codes[3].bitcast(FP8X4), scales=v_scales[:, 3 * P :], in_=vt_bf[3])
         multiply(3)
 
-        y_bf = sb.tile([P, Q, PACK], BF16, name="y_bf", align_bytes=64)
-        nc.vector.tensor_copy(y_bf[:, :P, :], acc[0][:].rearrange("p r q -> p q r"))
-        nc.scalar.copy(y_bf[:, P:, :], acc[1][:].rearrange("p r q -> p q r"))
+        y_bf = [sb.tile([P, P, PACK], BF16, name=f"y_bf{h}", align_bytes=64) for h in range(HALVES)]
+        nc.vector.tensor_copy(y_bf[0][:], acc[0][:].rearrange("p r q -> p q r"))
+        nc.scalar.copy(y_bf[1][:], acc[1][:].rearrange("p r q -> p q r"))
+        leave_bank(0, 3, PACK, nc.vector.tensor_copy)
+        leave_bank(1, 3, PACK, nc.scalar.copy)
         store_planes(3, PACK)
         y_codes = sb.tile([P, Q], U32, name="y_codes", align_bytes=64)
         y_scales = sb.tile([P, Q], U8, name="y_scales", align_bytes=64)
-        nc.vector.quantize_mx(out=y_codes[:].bitcast(FP8X4), scales=y_scales[:], in_=y_bf[:].rearrange("p q r -> p (q r)"))
+        for h in range(HALVES):
+            cols = slice(h * P, (h + 1) * P)
+            nc.vector.quantize_mx(out=y_codes[:, cols].bitcast(FP8X4), scales=y_scales[:, cols], in_=y_bf[h][:].rearrange("p q r -> p (q r)"))
 
         nc.sync.dma_start(out_1[0].rearrange("p c r -> p (c r)").bitcast(I32), y_codes[:].bitcast(I32))
         for quad in range(4):

@@ -22,6 +22,7 @@ P = 128
 PACK = 4
 HALVES = Q // P
 BIAS_WINDOW = 704
+CHUNKS = (0, 640, 1536, T)
 
 
 def tile_attend_bucketbias_pl_kernel(tc, query, keys_words, keys_scales, bias, size, vals, offs, offs2, out_0, out_1, out_2):
@@ -33,49 +34,56 @@ def tile_attend_bucketbias_pl_kernel(tc, query, keys_words, keys_scales, bias, s
 
         slot_tok = sb.tile([P, I // 16], U16, name="slot_tok")
         slot_bkt = sb.tile([P, I // 16], U16, name="slot_bkt")
-        key_words = sb.tile([P, T], U16, name="key_words", align_bytes=64)
-        key_scales = sb.tile([P, T], U8, name="key_scales", align_bytes=64)
+        key_scales = sb.tile([P, T], U8, name="key_scales", tag="rest0", align_bytes=64)
+        bias_sb = [
+            sb.tile([P, BIAS_WINDOW], F32, name="bias_sb0", tag="plane1", align_bytes=64),
+            sb.tile([P, BIAS_WINDOW], F32, name="bias_sb1", tag="plane3", align_bytes=64),
+        ]
+        key_words = sb.tile([P, T], U16, name="key_words", tag="plane2", align_bytes=64)
         q_raw = sb.tile([P, PACK, Q], F32, name="q_raw", tag="q_raw", align_bytes=64)
-        bias_sb = [sb.tile([P, BIAS_WINDOW], F32, name=f"bias_sb{h}") for h in range(HALVES)]
-        size_col = sb.tile([P, PACK], F32, name="size_col")
-        val_planes = [sb.tile([P, T], F32, name=f"val_plane{r}", tag=f"plane{r}", align_bytes=64) for r in range(1, PACK)]
-        val_chunks = [sb.tile([P, T // 2], F32, name=f"val_chunk{c}") for c in range(2)]
+        kg_scales = sb.tile([P, I], U8, name="kg_scales", align_bytes=64)
         ident = sb.tile([P, P], F32, name="ident")
 
-        nc.gpsimd.memset(key_scales[:].bitcast(I32), 0)
+        nc.gpsimd.memset(key_scales[:112, :].bitcast(I32), 0)
         for h in range(HALVES):
             nc.vector.memset(bias_sb[h][:, U:], 0.0)
 
+        nc.vector.memset(kg_scales[:].bitcast(I32), 0)
         make_identity(nc, ident[:])
 
-        nc.sync.dma_start(slot_bkt[:], offs2)
-        nc.sync.dma_start(bias_sb[0][:, :U], bias[:P, :])
-        nc.sync.dma_start(slot_tok[:], offs)
-        nc.sync.dma_start(key_words[:].bitcast(I32), keys_words[0].bitcast(I32))
-        for row in range(4):
-            nc.sync.dma_start(key_scales[row:P:32, :].bitcast(I32), keys_scales[0][row:16:4, :].bitcast(I32))
-        nc.sync.dma_start(q_raw[:], query.rearrange("(p t) q -> p t q", t=PACK))
         vals_dealt = vals.rearrange("(p r) t -> p r t", r=PACK)
-        for c in range(2):
-            nc.sync.dma_start(val_chunks[c][:], vals_dealt[:, 0, c * (T // 2) : (c + 1) * (T // 2)])
-            if c == 0:
-                nc.sync.dma_start(bias_sb[1][:, :U], bias[P:, :])
-        for r in range(1, PACK):
-            nc.sync.dma_start(val_planes[r - 1][:], vals_dealt[:, r, :])
-            if r == 1:
-                nc.sync.dma_start(size_col[:], size.rearrange("o (p t) -> (o p) t", t=PACK))
+        val_chunks = [sb.tile([P, CHUNKS[1]], F32, name="val_chunk0")[:]]
+        size_col = sb.tile([P, PACK], F32, name="size_col")
+        nc.sync.dma_start(slot_tok[:], offs)
+        nc.sync.dma_start(key_scales[112:, :].bitcast(I32), keys_scales[0].bitcast(I32))
+        nc.sync.dma_start(bias_sb[0][:, :U], bias[:P, :])
+        nc.sync.dma_start(slot_bkt[:], offs2)
+        nc.sync.dma_start(size_col[:], size.rearrange("o (p t) -> (o p) t", t=PACK))
+        nc.sync.dma_start(q_raw[:], query.rearrange("(p t) q -> p t q", t=PACK))
+        nc.sync.dma_start(key_words[:].bitcast(I32), keys_words[0].bitcast(I32))
+        nc.sync.dma_start(bias_sb[1][:, :U], bias[P:, :])
+        nc.sync.dma_start(val_chunks[0], vals_dealt[:, 0, : CHUNKS[1]])
+
+        kg_spread = sb.tile([P, I], U8, name="kg_spread", align_bytes=64)
+        nc.vector.tensor_copy(kg_spread[:], key_scales[:].indirect(slot_tok[:]))
+        for row in range(4):
+            nc.sync.dma_start(kg_scales[row:P:32, :].bitcast(I32), kg_spread[112 + row : P : 4, :].bitcast(I32))
+        rest0 = sb.tile([P, T - CHUNKS[1]], F32, name="rest0", tag="rest0", align_bytes=64)
+        for c in (1, 2):
+            val_chunks.append(rest0[:, CHUNKS[c] - CHUNKS[1] : CHUNKS[c + 1] - CHUNKS[1]])
+            nc.sync.dma_start(val_chunks[c], vals_dealt[:, 0, CHUNKS[c] : CHUNKS[c + 1]])
+
+        bias_g = [sb.tile([P, I], F32, name="bias_g0", align_bytes=64)]
+        nc.vector.tensor_copy(bias_g[0][:], bias_sb[0][:].indirect(slot_bkt[:]))
+        kg_words = sb.tile([P, I], U16, name="kg_words", align_bytes=64)
+        nc.vector.tensor_copy(kg_words[:], key_words[:].indirect(slot_tok[:]))
 
         size_rows = ps.tile([P, I], F32, name="size_rows")
         size_places = size_rows[:].rearrange("p (u g x t) -> p t g u x", u=2, x=4, t=PACK)
         for t in range(PACK):
             nc.tensor.transpose(size_places[:, t], size_col[:, t : t + 1].to_broadcast([P, P]), ident[:])
 
-        kg_words = sb.tile([P, I], U16, name="kg_words", align_bytes=64)
-        kg_scales = sb.tile([P, I], U8, name="kg_scales", align_bytes=64)
-        nc.vector.tensor_copy(kg_words[:], key_words[:].indirect(slot_tok[:]))
-        nc.vector.tensor_copy(kg_scales[:], key_scales[:].indirect(slot_tok[:]))
-
-        q_bf = sb.tile([P, Q, PACK], BF16, name="q_bf", tag="q_bf", align_bytes=64)
+        q_bf = sb.tile([P, Q, PACK], BF16, name="q_bf", align_bytes=64)
         nc.scalar.activation(
             q_bf[:].rearrange("p (c i) t -> p c t i", i=4),
             q_raw[:].rearrange("p t (c i) -> p c t i", i=4),
@@ -84,6 +92,10 @@ def tile_attend_bucketbias_pl_kernel(tc, query, keys_words, keys_scales, bias, s
         q_codes = sb.tile([P, Q], U32, name="q_codes", align_bytes=64)
         q_scales = sb.tile([P, Q], U8, name="q_scales", align_bytes=64)
         nc.vector.quantize_mx(out=q_codes[:].bitcast(FP8X4), scales=q_scales[:], in_=q_bf[:].rearrange("p q t -> p (q t)"))
+
+        val_planes = [sb.tile([P, T], F32, name=f"val_plane{r}", tag=f"plane{r}", align_bytes=64) for r in range(1, PACK)]
+        for r in range(1, PACK):
+            nc.sync.dma_start(val_planes[r - 1][:], vals_dealt[:, r, :])
 
         scores = [ps.tile([P, I], F32, name=f"scores{h}", tag=f"bank{h}") for h in range(HALVES)]
         for h in range(HALVES):
@@ -97,12 +109,8 @@ def tile_attend_bucketbias_pl_kernel(tc, query, keys_words, keys_scales, bias, s
                 stop=True,
             )
 
-        bias_g = [
-            sb.tile([P, I], F32, name="bias_g0", align_bytes=64),
-            sb.tile([P, I], F32, name="bias_g1", tag="q_raw", align_bytes=64),
-        ]
-        for h in range(HALVES):
-            nc.vector.tensor_copy(bias_g[h][:], bias_sb[h][:].indirect(slot_bkt[:]))
+        bias_g.append(sb.tile([P, I], F32, name="bias_g1", tag="q_raw", align_bytes=64))
+        nc.vector.tensor_copy(bias_g[1][:], bias_sb[1][:].indirect(slot_bkt[:]))
 
         def dealt(ap):
             return ap.rearrange("p (u g x) -> p g u x", u=2, x=16)
@@ -120,8 +128,8 @@ def tile_attend_bucketbias_pl_kernel(tc, query, keys_words, keys_scales, bias, s
         wt_bf = early_bf[:, : Q * PACK]
         vt_bf = [early_bf[:, Q * PACK : Q * PACK + I], early_bf[:, Q * PACK + I :], late_bf[:, :I], late_bf[:, I:]]
         plane0_bf = sb.tile([P, T], BF16, name="plane0_bf", tag="plane0_bf", align_bytes=64)
-        for c in range(2):
-            nc.scalar.activation(plane0_bf[:, c * (T // 2) : (c + 1) * (T // 2)], val_chunks[c][:], ACT.Copy)
+        for c in range(3):
+            nc.scalar.activation(plane0_bf[:, CHUNKS[c] : CHUNKS[c + 1]], val_chunks[c], ACT.Copy)
 
         def gather_plane0_half(c):
             n = I // 2
@@ -131,14 +139,15 @@ def tile_attend_bucketbias_pl_kernel(tc, query, keys_words, keys_scales, bias, s
         gather_plane0_half(0)
 
         logits = [sb.tile([P, I], F32, name=f"logits{h}") for h in range(HALVES)]
-        probs_all = sb.tile([P, HALVES, I], F32, name="probs_all", align_bytes=64)
+        probs_all = sb.tile([P, HALVES, I], F32, name="probs_all", tag="rest0", align_bytes=64)
         probs = [probs_all[:, h, :] for h in range(HALVES)]
         neg_max = [sb.tile([P, 1], F32, name=f"neg_max{h}") for h in range(HALVES)]
         row_sum = sb.tile([P, HALVES], F32, name="row_sum")
         inv_sum = sb.tile([P, HALVES], F32, name="inv_sum")
         minus_one = sb.tile([P, 1], F32, name="minus_one")
         nc.gpsimd.memset(minus_one[:], -1.0)
-        w_bf = [sb.tile([P, I], BF16, name=f"w_bf{h}", align_bytes=64) for h in range(HALVES)]
+        w_all = sb.tile([P, HALVES * I], BF16, name="w_all", tag="plane1", align_bytes=64)
+        w_bf = [w_all[:, h * I : (h + 1) * I] for h in range(HALVES)]
         for h in range(HALVES):
             nc.vector.tensor_tensor(
                 logits[h][:].rearrange("p (u g x) -> p u g x", u=2, x=16),
@@ -150,6 +159,7 @@ def tile_attend_bucketbias_pl_kernel(tc, query, keys_words, keys_scales, bias, s
             nc.vector.tensor_reduce(neg_max[h][:], logits[h][:], AX.X, ALU.max, negate=True)
             nc.scalar.activation(probs[h], logits[h][:], ACT.Exp, bias=neg_max[h][:], accum_out=row_sum[:, h : h + 1])
             nc.gpsimd.tensor_tensor(inv_sum[:, h : h + 1], row_sum[:, h : h + 1], minus_one[:], ALU.pow)
+
         gather_plane0_half(1)
 
         def gather_plane(r):
@@ -160,14 +170,14 @@ def tile_attend_bucketbias_pl_kernel(tc, query, keys_words, keys_scales, bias, s
         turn_words(vg_bf[0][:], vt_bf[0])
         for h in range(HALVES):
             nc.vector.scalar_tensor_tensor(
-                w_bf[h][:],
+                w_bf[h],
                 probs[h],
                 inv_sum[:, h : h + 1],
                 size_rows[:],
                 ALU.mult,
                 ALU.mult,
             )
-            turn_words(w_bf[h][:], wt_bf[:, h * P * PACK : (h + 1) * P * PACK])
+            turn_words(w_bf[h], wt_bf[:, h * P * PACK : (h + 1) * P * PACK])
         gather_plane(2)
 
         early_codes = sb.tile([P, Q + 2 * P], U32, name="early_codes", tag="plane2", align_bytes=64)

@@ -22,7 +22,7 @@ P = 128
 PACK = 4
 HALVES = Q // P
 BIAS_WINDOW = 704
-CHUNKS = (0, 640, 1536, T)
+CHUNKS = (0, 768, 1408, T)
 
 
 def tile_attend_bucketbias_pl_kernel(tc, query, keys_words, keys_scales, bias, size, vals, offs, offs2, out_0, out_1, out_2):
@@ -209,21 +209,23 @@ def tile_attend_bucketbias_pl_kernel(tc, query, keys_words, keys_scales, bias, s
         def leave_bank(h, first, end, copy):
             copy(y[:, first:end, h * P : (h + 1) * P], acc[h][:, first:end, :])
 
-        def store_planes(first, end):
-            nc.sync.dma_start(out_dealt[:, first:end, :], y[:, first:end, :])
+        def store_half(h, r):
+            nc.sync.dma_start(out_dealt[:, r, h * P : (h + 1) * P], y[:, r, h * P : (h + 1) * P])
 
         multiply(0)
         multiply(1)
         for h in range(HALVES):
             leave_bank(h, 0, 2, nc.scalar.copy)
-        store_planes(0, 2)
+            for r in range(2):
+                store_half(h, r)
         vg_bf.append(sb.tile([P, I], BF16, name="vg_bf3", align_bytes=64))
         gather_plane(3)
         nc.vector.quantize_mx(out=v_codes[2].bitcast(FP8X4), scales=v_scales[:, 2 * P : 3 * P], in_=vt_bf[2])
         multiply(2)
         leave_bank(0, 2, 3, nc.vector.tensor_copy)
         leave_bank(1, 2, 3, nc.scalar.copy)
-        store_planes(2, 3)
+        for h in range(HALVES):
+            store_half(h, 2)
         nc.vector.quantize_mx(out=v_codes[3].bitcast(FP8X4), scales=v_scales[:, 3 * P :], in_=vt_bf[3])
         multiply(3)
 
@@ -232,14 +234,15 @@ def tile_attend_bucketbias_pl_kernel(tc, query, keys_words, keys_scales, bias, s
         nc.scalar.copy(y_bf[1][:], acc[1][:].rearrange("p r q -> p q r"))
         leave_bank(0, 3, PACK, nc.vector.tensor_copy)
         leave_bank(1, 3, PACK, nc.scalar.copy)
-        store_planes(3, PACK)
+        for h in range(HALVES):
+            store_half(h, 3)
         y_codes = sb.tile([P, Q], U32, name="y_codes", align_bytes=64)
         y_scales = sb.tile([P, Q], U8, name="y_scales", align_bytes=64)
         for h in range(HALVES):
             cols = slice(h * P, (h + 1) * P)
             nc.vector.quantize_mx(out=y_codes[:, cols].bitcast(FP8X4), scales=y_scales[:, cols], in_=y_bf[h][:].rearrange("p q r -> p (q r)"))
+            nc.sync.dma_start(out_1[0].rearrange("p c r -> p (c r)").bitcast(I32)[:, cols], y_codes[:, cols].bitcast(I32))
 
-        nc.sync.dma_start(out_1[0].rearrange("p c r -> p (c r)").bitcast(I32), y_codes[:].bitcast(I32))
         for quad in range(4):
             queue = nc.scalar if quad % 2 == 0 else nc.sync
             queue.dma_start(

@@ -21,8 +21,8 @@ AX = mybir.AxisListType
 P = 128
 PACK = 4
 HALVES = Q // P
-BIAS_WINDOW = 704
-CHUNKS = (0, 768, 1408, T)
+LEAD = 768
+VECTOR_SLOTS = (0, I, I, 320)
 
 
 def tile_attend_bucketbias_pl_kernel(tc, query, keys_words, keys_scales, bias, size, vals, offs, offs2, out_0, out_1, out_2):
@@ -34,68 +34,75 @@ def tile_attend_bucketbias_pl_kernel(tc, query, keys_words, keys_scales, bias, s
 
         slot_tok = sb.tile([P, I // 16], U16, name="slot_tok")
         slot_bkt = sb.tile([P, I // 16], U16, name="slot_bkt")
-        key_scales = sb.tile([P, T], U8, name="key_scales", tag="rest0", align_bytes=64)
+        key_scales = sb.tile([P, T], U8, name="key_scales", tag="plane0", align_bytes=64)
         bias_sb = [
-            sb.tile([P, BIAS_WINDOW], F32, name="bias_sb0", tag="plane1", align_bytes=64),
-            sb.tile([P, BIAS_WINDOW], F32, name="bias_sb1", tag="plane3", align_bytes=64),
+            sb.tile([P, U], F32, name="bias_sb0", align_bytes=64),
+            sb.tile([P, U], F32, name="bias_sb1", align_bytes=64),
         ]
-        key_words = sb.tile([P, T], U16, name="key_words", tag="plane2", align_bytes=64)
-        q_raw = sb.tile([P, PACK, Q], F32, name="q_raw", tag="q_raw", align_bytes=64)
+        key_words = sb.tile([P, T], U16, name="key_words", tag="plane1", align_bytes=64)
+        q_raw = sb.tile([P, PACK, Q], F32, name="q_raw", tag="plane2", align_bytes=64)
         kg_scales = sb.tile([P, I], U8, name="kg_scales", align_bytes=64)
         ident = sb.tile([P, P], F32, name="ident")
 
         nc.gpsimd.memset(key_scales[:112, :].bitcast(I32), 0)
-        for h in range(HALVES):
-            nc.vector.memset(bias_sb[h][:, U:], 0.0)
-
         nc.vector.memset(kg_scales[:].bitcast(I32), 0)
         make_identity(nc, ident[:])
 
         vals_dealt = vals.rearrange("(p r) t -> p r t", r=PACK)
-        val_chunks = [sb.tile([P, CHUNKS[1]], F32, name="val_chunk0")[:]]
+        lead = sb.tile([P, LEAD], F32, name="lead", tag="plane3", align_bytes=64)
         size_col = sb.tile([P, PACK], F32, name="size_col")
         nc.sync.dma_start(slot_tok[:], offs)
         nc.sync.dma_start(key_scales[112:, :].bitcast(I32), keys_scales[0].bitcast(I32))
-        nc.sync.dma_start(bias_sb[0][:, :U], bias[:P, :])
+        nc.sync.dma_start(bias_sb[0][:], bias[:P, :])
         nc.sync.dma_start(slot_bkt[:], offs2)
         nc.sync.dma_start(size_col[:], size.rearrange("o (p t) -> (o p) t", t=PACK))
-        nc.sync.dma_start(q_raw[:], query.rearrange("(p t) q -> p t q", t=PACK))
         nc.sync.dma_start(key_words[:].bitcast(I32), keys_words[0].bitcast(I32))
-        nc.sync.dma_start(bias_sb[1][:, :U], bias[P:, :])
-        nc.sync.dma_start(val_chunks[0], vals_dealt[:, 0, : CHUNKS[1]])
+        nc.sync.dma_start(q_raw[:], query.rearrange("(p t) q -> p t q", t=PACK))
+        nc.sync.dma_start(bias_sb[1][:], bias[P:, :])
+        nc.sync.dma_start(lead[:], vals_dealt[:, 0, :LEAD])
 
         kg_spread = sb.tile([P, I], U8, name="kg_spread", align_bytes=64)
         nc.vector.tensor_copy(kg_spread[:], key_scales[:].indirect(slot_tok[:]))
         for row in range(4):
             nc.sync.dma_start(kg_scales[row:P:32, :].bitcast(I32), kg_spread[112 + row : P : 4, :].bitcast(I32))
-        rest0 = sb.tile([P, T - CHUNKS[1]], F32, name="rest0", tag="rest0", align_bytes=64)
-        for c in (1, 2):
-            val_chunks.append(rest0[:, CHUNKS[c] - CHUNKS[1] : CHUNKS[c + 1] - CHUNKS[1]])
-            nc.sync.dma_start(val_chunks[c], vals_dealt[:, 0, CHUNKS[c] : CHUNKS[c + 1]])
+        val_planes = [sb.tile([P, T], F32, name="val_plane0", tag="plane0", align_bytes=64)]
+        nc.sync.dma_start(val_planes[0][:, LEAD:], vals_dealt[:, 0, LEAD:])
 
-        bias_g = [sb.tile([P, I], F32, name="bias_g0", align_bytes=64)]
-        nc.vector.tensor_copy(bias_g[0][:], bias_sb[0][:].indirect(slot_bkt[:]))
+        bias_g = [sb.tile([P, I], F32, name=f"bias_g{h}", align_bytes=64) for h in range(HALVES)]
+
+        def gather_bias(h):
+            n = I // 2
+            for c in range(2):
+                offsets = slot_bkt[:, c * n // 16 : (c + 1) * n // 16]
+                nc.scalar.activation(bias_g[h][:, c * n : (c + 1) * n], bias_sb[h][:].indirect(offsets), ACT.Copy)
+
+        gather_bias(0)
+
         kg_words = sb.tile([P, I], U16, name="kg_words", align_bytes=64)
         nc.vector.tensor_copy(kg_words[:], key_words[:].indirect(slot_tok[:]))
 
-        size_rows = ps.tile([P, I], F32, name="size_rows")
-        size_places = size_rows[:].rearrange("p (u g x t) -> p t g u x", u=2, x=4, t=PACK)
-        for t in range(PACK):
-            nc.tensor.transpose(size_places[:, t], size_col[:, t : t + 1].to_broadcast([P, P]), ident[:])
-
         q_bf = sb.tile([P, Q, PACK], BF16, name="q_bf", align_bytes=64)
-        nc.scalar.activation(
+        nc.vector.tensor_copy(
             q_bf[:].rearrange("p (c i) t -> p c t i", i=4),
             q_raw[:].rearrange("p t (c i) -> p c t i", i=4),
-            ACT.Copy,
         )
         q_codes = sb.tile([P, Q], U32, name="q_codes", align_bytes=64)
         q_scales = sb.tile([P, Q], U8, name="q_scales", align_bytes=64)
         nc.vector.quantize_mx(out=q_codes[:].bitcast(FP8X4), scales=q_scales[:], in_=q_bf[:].rearrange("p q t -> p (q t)"))
+        gather_bias(1)
+        nc.vector.tensor_copy(val_planes[0][:, :LEAD], lead[:])
 
-        val_planes = [sb.tile([P, T], F32, name=f"val_plane{r}", tag=f"plane{r}", align_bytes=64) for r in range(1, PACK)]
+        def load_plane(r):
+            val_planes.append(sb.tile([P, T], F32, name=f"val_plane{r}", tag=f"plane{r}", align_bytes=64))
+            nc.sync.dma_start(val_planes[r][:], vals_dealt[:, r, :])
+
         for r in range(1, PACK):
-            nc.sync.dma_start(val_planes[r - 1][:], vals_dealt[:, r, :])
+            load_plane(r)
+
+        size_rows = ps.tile([P, I], F32, name="size_rows")
+        size_places = size_rows[:].rearrange("p (u c b) -> p u b c", u=2, b=2)
+        for t in range(PACK):
+            nc.tensor.transpose(size_places[:, t // 2, t % 2], size_col[:, t : t + 1].to_broadcast([P, P]), ident[:])
 
         scores = [ps.tile([P, I], F32, name=f"scores{h}", tag=f"bank{h}") for h in range(HALVES)]
         for h in range(HALVES):
@@ -109,89 +116,83 @@ def tile_attend_bucketbias_pl_kernel(tc, query, keys_words, keys_scales, bias, s
                 stop=True,
             )
 
-        bias_g.append(sb.tile([P, I], F32, name="bias_g1", tag="q_raw", align_bytes=64))
-        nc.vector.tensor_copy(bias_g[1][:], bias_sb[1][:].indirect(slot_bkt[:]))
-
-        def dealt(ap):
-            return ap.rearrange("p (u g x) -> p g u x", u=2, x=16)
-
-        def turn_words(src_bf, dst_bf):
-            words = src_bf.bitcast(F32)
+        def turn_words(word_sets, dst_bf, copy):
             bank = turn.tile([P, 2, P], F32, name="turn_bank")
             for u in range(2):
-                nc.tensor.transpose(bank[:, u, :], words[:, u * P : (u + 1) * P], ident[:])
-            nc.scalar.copy(dst_bf.bitcast(F32).rearrange("p (c u) -> p c u", u=2), bank[:].rearrange("p u c -> p c u"))
+                nc.tensor.transpose(bank[:, u, :], word_sets[u], ident[:])
+            copy(dst_bf.bitcast(F32).rearrange("p (c u) -> p c u", u=2), bank[:].rearrange("p u c -> p c u"))
 
-        vg_bf = [sb.tile([P, I], BF16, name=f"vg_bf{r}", align_bytes=64) for r in range(PACK - 1)]
-        early_bf = sb.tile([P, Q * PACK + 2 * I], BF16, name="early_bf", tag="early_bf", align_bytes=64)
-        late_bf = sb.tile([P, 2 * I], BF16, name="late_bf", align_bytes=64)
-        wt_bf = early_bf[:, : Q * PACK]
-        vt_bf = [early_bf[:, Q * PACK : Q * PACK + I], early_bf[:, Q * PACK + I :], late_bf[:, :I], late_bf[:, I:]]
-        plane0_bf = sb.tile([P, T], BF16, name="plane0_bf", tag="plane0_bf", align_bytes=64)
-        for c in range(3):
-            nc.scalar.activation(plane0_bf[:, CHUNKS[c] : CHUNKS[c + 1]], val_chunks[c], ACT.Copy)
+        vg_bf = [sb.tile([P, I], BF16, name=f"vg_bf{r}", align_bytes=64) for r in range(PACK)]
+        vt_bf = {r: sb.tile([P, I], BF16, name=f"vt_bf{r}", align_bytes=64)[:] for r in (1, 3)}
 
-        def gather_plane0_half(c):
-            n = I // 2
-            offsets = slot_tok[:, c * n // 16 : (c + 1) * n // 16]
-            nc.scalar.activation(dealt(vg_bf[0][:])[:, c * 8 : (c + 1) * 8], plane0_bf[:].indirect(offsets), ACT.Copy)
+        def gather_plane(r):
+            n = VECTOR_SLOTS[r]
+            if n > 0:
+                nc.vector.tensor_copy(vg_bf[r][:, :n], val_planes[r][:].indirect(slot_tok[:, : n // 16]))
+            if n < I:
+                nc.scalar.activation(vg_bf[r][:, n:], val_planes[r][:].indirect(slot_tok[:, n // 16 :]), ACT.Copy)
 
-        gather_plane0_half(0)
+        def turn_plane(r):
+            words = vg_bf[r][:].bitcast(F32)
+            turn_words([words[:, u::2] for u in range(2)], vt_bf[r], nc.scalar.copy)
 
-        logits = [sb.tile([P, I], F32, name=f"logits{h}") for h in range(HALVES)]
-        probs_all = sb.tile([P, HALVES, I], F32, name="probs_all", tag="rest0", align_bytes=64)
-        probs = [probs_all[:, h, :] for h in range(HALVES)]
+        v_codes = {}
+        v_scales = [sb.tile([P, P], U8, name=f"v_scales{r}", align_bytes=64) for r in range(PACK)]
+        w_scales = sb.tile([P, Q], U8, name="w_scales", align_bytes=64)
+
+        def quantise_plane(r):
+            nc.vector.quantize_mx(out=v_codes[r].bitcast(FP8X4), scales=v_scales[r][:], in_=vt_bf[r])
+
+        gather_plane(0)
+
+        logits = [sb.tile([P, I], F32, name=f"logits{h}", tag=f"logits{h}", align_bytes=64) for h in range(HALVES)]
         neg_max = [sb.tile([P, 1], F32, name=f"neg_max{h}") for h in range(HALVES)]
         row_sum = sb.tile([P, HALVES], F32, name="row_sum")
         inv_sum = sb.tile([P, HALVES], F32, name="inv_sum")
         minus_one = sb.tile([P, 1], F32, name="minus_one")
         nc.gpsimd.memset(minus_one[:], -1.0)
-        w_all = sb.tile([P, HALVES * I], BF16, name="w_all", tag="plane1", align_bytes=64)
-        w_bf = [w_all[:, h * I : (h + 1) * I] for h in range(HALVES)]
         for h in range(HALVES):
             nc.vector.tensor_tensor(
-                logits[h][:].rearrange("p (u g x) -> p u g x", u=2, x=16),
-                scores[h][:].rearrange("p (g u x) -> p u g x", u=2, x=16),
-                bias_g[h][:].rearrange("p (g u x) -> p u g x", u=2, x=16),
+                logits[h][:].rearrange("p (u c b) -> p u c b", u=2, b=2),
+                scores[h][:].rearrange("p (c u b) -> p u c b", u=2, b=2),
+                bias_g[h][:].rearrange("p (c u b) -> p u c b", u=2, b=2),
                 ALU.add,
             )
         for h in range(HALVES):
             nc.vector.tensor_reduce(neg_max[h][:], logits[h][:], AX.X, ALU.max, negate=True)
+
+        def exponentiate(h):
             nc.scalar.activation(probs[h], logits[h][:], ACT.Exp, bias=neg_max[h][:], accum_out=row_sum[:, h : h + 1])
             nc.gpsimd.tensor_tensor(inv_sum[:, h : h + 1], row_sum[:, h : h + 1], minus_one[:], ALU.pow)
 
-        gather_plane0_half(1)
-
-        def gather_plane(r):
-            nc.vector.tensor_copy(dealt(vg_bf[r][:]), val_planes[r - 1][:].indirect(slot_tok[:]))
-            turn_words(vg_bf[r][:], vt_bf[r])
-
-        gather_plane(1)
-        turn_words(vg_bf[0][:], vt_bf[0])
+        probs = [sb.tile([P, I], F32, name=f"probs{h}", align_bytes=64)[:] for h in range(HALVES)]
         for h in range(HALVES):
-            nc.vector.scalar_tensor_tensor(
-                w_bf[h],
-                probs[h],
-                inv_sum[:, h : h + 1],
-                size_rows[:],
-                ALU.mult,
-                ALU.mult,
-            )
-            turn_words(w_bf[h], wt_bf[:, h * P * PACK : (h + 1) * P * PACK])
-        gather_plane(2)
+            exponentiate(h)
+        vt_bf[0] = sb.tile([P, I], BF16, name="vt_bf0", tag="logits1", align_bytes=64)[:]
+        turn_plane(0)
+        gather_plane(1)
+        w_all = sb.tile([P, HALVES * I], BF16, name="w_all", tag="plane1", align_bytes=64)
+        w_bf = [w_all[:, h * I : (h + 1) * I] for h in range(HALVES)]
+        wt_bf = sb.tile([P, Q * PACK], BF16, name="wt_bf", align_bytes=64)
 
+        def weigh(h):
+            nc.vector.scalar_tensor_tensor(w_bf[h], probs[h], inv_sum[:, h : h + 1], size_rows[:], ALU.mult, ALU.mult)
+            words = w_bf[h].bitcast(F32)
+            turn_words([words[:, u * P : (u + 1) * P] for u in range(2)], wt_bf[:, h * P * PACK : (h + 1) * P * PACK], nc.scalar.copy)
+
+        turn_plane(1)
+        weigh(0)
+        weigh(1)
+        gather_plane(2)
         early_codes = sb.tile([P, Q + 2 * P], U32, name="early_codes", tag="plane2", align_bytes=64)
-        late_codes = sb.tile([P, 2 * P], U32, name="late_codes", tag="plane3", align_bytes=64)
-        all_scales = sb.tile([P, Q + PACK * P], U8, name="all_scales", align_bytes=64)
-        w_scales = all_scales[:, :Q]
-        v_scales = all_scales[:, Q:]
         w_codes = early_codes[:, :Q]
-        v_codes = [early_codes[:, Q : Q + P], early_codes[:, Q + P :], late_codes[:, :P], late_codes[:, P:]]
-        nc.vector.quantize_mx(out=early_codes[:, Q:].bitcast(FP8X4), scales=v_scales[:, : 2 * P], in_=early_bf[:, Q * PACK :])
-        nc.vector.quantize_mx(out=w_codes.bitcast(FP8X4), scales=w_scales, in_=wt_bf)
+        v_codes[0] = early_codes[:, Q : Q + P]
+        v_codes[1] = early_codes[:, Q + P :]
+        quantise_plane(0)
+        quantise_plane(1)
+        nc.vector.quantize_mx(out=w_codes.bitcast(FP8X4), scales=w_scales[:], in_=wt_bf[:])
 
         out_dealt = out_0.rearrange("(p r) q -> p r q", r=PACK)
-        y = sb.tile([P, PACK, Q], F32, name="y")
         acc = [ps.tile([P, PACK, P], F32, name=f"acc{h}", tag=f"bank{h}") for h in range(HALVES)]
 
         def multiply(r):
@@ -199,7 +200,7 @@ def tile_attend_bucketbias_pl_kernel(tc, query, keys_words, keys_scales, bias, s
                 nc.tensor.matmul_mx(
                     out=acc[h][:, r, :],
                     lhsT=v_codes[r].bitcast(FP8X4),
-                    lhsT_scale=v_scales[:, r * P : (r + 1) * P],
+                    lhsT_scale=v_scales[r][:],
                     rhs=w_codes[:, h * P : (h + 1) * P].bitcast(FP8X4),
                     rhs_scale=w_scales[:, h * P : (h + 1) * P],
                     start=True,
@@ -209,24 +210,25 @@ def tile_attend_bucketbias_pl_kernel(tc, query, keys_words, keys_scales, bias, s
         def leave_bank(h, first, end, copy):
             copy(y[:, first:end, h * P : (h + 1) * P], acc[h][:, first:end, :])
 
-        def store_half(h, r):
-            nc.sync.dma_start(out_dealt[:, r, h * P : (h + 1) * P], y[:, r, h * P : (h + 1) * P])
-
         multiply(0)
         multiply(1)
-        for h in range(HALVES):
-            leave_bank(h, 0, 2, nc.scalar.copy)
-            for r in range(2):
-                store_half(h, r)
-        vg_bf.append(sb.tile([P, I], BF16, name="vg_bf3", align_bytes=64))
         gather_plane(3)
-        nc.vector.quantize_mx(out=v_codes[2].bitcast(FP8X4), scales=v_scales[:, 2 * P : 3 * P], in_=vt_bf[2])
+        behind_plane3 = sb.tile([P, PACK * Q + I // 2], F32, name="behind_plane3", tag="plane3", align_bytes=64)
+        y = behind_plane3[:, : PACK * Q].rearrange("p (r q) -> p r q", r=PACK)
+        vt_bf[2] = behind_plane3[:, PACK * Q :].bitcast(BF16)
+        for r in (2, 3):
+            v_codes[r] = sb.tile([P, P], U32, name=f"v_codes{r}", align_bytes=64)[:]
+        turn_plane(2)
+        turn_plane(3)
+        leave_bank(0, 0, 2, nc.vector.tensor_copy)
+        leave_bank(1, 0, 2, nc.scalar.copy)
+        nc.sync.dma_start(out_dealt[:, :2, :], y[:, :2, :])
+        quantise_plane(2)
         multiply(2)
-        leave_bank(0, 2, 3, nc.vector.tensor_copy)
-        leave_bank(1, 2, 3, nc.scalar.copy)
+        quantise_plane(3)
         for h in range(HALVES):
-            store_half(h, 2)
-        nc.vector.quantize_mx(out=v_codes[3].bitcast(FP8X4), scales=v_scales[:, 3 * P :], in_=vt_bf[3])
+            leave_bank(h, 2, 3, nc.scalar.copy)
+        nc.sync.dma_start(out_dealt[:, 2, :], y[:, 2, :])
         multiply(3)
 
         y_bf = [sb.tile([P, P, PACK], BF16, name=f"y_bf{h}", align_bytes=64) for h in range(HALVES)]
@@ -234,8 +236,7 @@ def tile_attend_bucketbias_pl_kernel(tc, query, keys_words, keys_scales, bias, s
         nc.scalar.copy(y_bf[1][:], acc[1][:].rearrange("p r q -> p q r"))
         leave_bank(0, 3, PACK, nc.vector.tensor_copy)
         leave_bank(1, 3, PACK, nc.scalar.copy)
-        for h in range(HALVES):
-            store_half(h, 3)
+        nc.sync.dma_start(out_dealt[:, 3, :], y[:, 3, :])
         y_codes = sb.tile([P, Q], U32, name="y_codes", align_bytes=64)
         y_scales = sb.tile([P, Q], U8, name="y_scales", align_bytes=64)
         for h in range(HALVES):

@@ -22,15 +22,17 @@ P = 128
 PACK = 4
 HALVES = Q // P
 LEAD = 768
-VECTOR_SLOTS = (0, I, I, 320)
+VECTOR_SLOTS = (0, I, 320, 320)
 
 
 def tile_attend_bucketbias_pl_kernel(tc, query, keys_words, keys_scales, bias, size, vals, offs, offs2, out_0, out_1, out_2):
     nc = tc.nc
     with ExitStack() as ctx:
         sb = ctx.enter_context(tc.tile_pool(name="sb", bufs=1))
+        room2 = ctx.enter_context(tc.tile_pool(name="room2", bufs=1))
+        room3 = ctx.enter_context(tc.tile_pool(name="room3", bufs=1))
         ps = ctx.enter_context(tc.psum_pool(name="ps", bufs=1))
-        turn = ctx.enter_context(tc.psum_pool(name="turn", bufs=3))
+        turn = ctx.enter_context(tc.psum_pool(name="turn", bufs=5))
 
         slot_tok = sb.tile([P, I // 16], U16, name="slot_tok")
         slot_bkt = sb.tile([P, I // 16], U16, name="slot_bkt")
@@ -40,7 +42,7 @@ def tile_attend_bucketbias_pl_kernel(tc, query, keys_words, keys_scales, bias, s
             sb.tile([P, U], F32, name="bias_sb1", align_bytes=64),
         ]
         key_words = sb.tile([P, T], U16, name="key_words", tag="plane1", align_bytes=64)
-        q_raw = sb.tile([P, PACK, Q], F32, name="q_raw", tag="plane2", align_bytes=64)
+        q_raw = room2.tile([P, PACK, Q], F32, name="q_raw", offset=0, align_bytes=64)
         kg_scales = sb.tile([P, I], U8, name="kg_scales", align_bytes=64)
         ident = sb.tile([P, P], F32, name="ident")
 
@@ -49,7 +51,7 @@ def tile_attend_bucketbias_pl_kernel(tc, query, keys_words, keys_scales, bias, s
         make_identity(nc, ident[:])
 
         vals_dealt = vals.rearrange("(p r) t -> p r t", r=PACK)
-        lead = sb.tile([P, LEAD], F32, name="lead", tag="plane3", align_bytes=64)
+        lead = room3.tile([P, LEAD], F32, name="lead", offset=0, align_bytes=64)
         size_col = sb.tile([P, PACK], F32, name="size_col")
         nc.sync.dma_start(slot_tok[:], offs)
         nc.sync.dma_start(key_scales[112:, :].bitcast(I32), keys_scales[0].bitcast(I32))
@@ -92,12 +94,11 @@ def tile_attend_bucketbias_pl_kernel(tc, query, keys_words, keys_scales, bias, s
         gather_bias(1)
         nc.vector.tensor_copy(val_planes[0][:, :LEAD], lead[:])
 
-        def load_plane(r):
-            val_planes.append(sb.tile([P, T], F32, name=f"val_plane{r}", tag=f"plane{r}", align_bytes=64))
-            nc.sync.dma_start(val_planes[r][:], vals_dealt[:, r, :])
-
+        val_planes.append(sb.tile([P, T], F32, name="val_plane1", tag="plane1", align_bytes=64))
+        val_planes.append(room2.tile([P, T], F32, name="val_plane2", offset=0, align_bytes=64))
+        val_planes.append(room3.tile([P, T], F32, name="val_plane3", offset=0, align_bytes=64))
         for r in range(1, PACK):
-            load_plane(r)
+            nc.sync.dma_start(val_planes[r][:], vals_dealt[:, r, :])
 
         size_rows = ps.tile([P, I], F32, name="size_rows")
         size_places = size_rows[:].rearrange("p (u c b) -> p u b c", u=2, b=2)
@@ -123,7 +124,7 @@ def tile_attend_bucketbias_pl_kernel(tc, query, keys_words, keys_scales, bias, s
             copy(dst_bf.bitcast(F32).rearrange("p (c u) -> p c u", u=2), bank[:].rearrange("p u c -> p c u"))
 
         vg_bf = [sb.tile([P, I], BF16, name=f"vg_bf{r}", align_bytes=64) for r in range(PACK)]
-        vt_bf = {r: sb.tile([P, I], BF16, name=f"vt_bf{r}", align_bytes=64)[:] for r in (1, 3)}
+        vt_bf = {r: sb.tile([P, I], BF16, name=f"vt_bf{r}", align_bytes=64)[:] for r in (2, 3)}
 
         def gather_plane(r):
             n = VECTOR_SLOTS[r]
@@ -137,11 +138,12 @@ def tile_attend_bucketbias_pl_kernel(tc, query, keys_words, keys_scales, bias, s
             turn_words([words[:, u::2] for u in range(2)], vt_bf[r], nc.scalar.copy)
 
         v_codes = {}
-        v_scales = [sb.tile([P, P], U8, name=f"v_scales{r}", align_bytes=64) for r in range(PACK)]
+        v_scales_all = sb.tile([P, PACK * P], U8, name="v_scales", align_bytes=64)
+        v_scales = [v_scales_all[:, r * P : (r + 1) * P] for r in range(PACK)]
         w_scales = sb.tile([P, Q], U8, name="w_scales", align_bytes=64)
 
         def quantise_plane(r):
-            nc.vector.quantize_mx(out=v_codes[r].bitcast(FP8X4), scales=v_scales[r][:], in_=vt_bf[r])
+            nc.vector.quantize_mx(out=v_codes[r].bitcast(FP8X4), scales=v_scales[r], in_=vt_bf[r])
 
         gather_plane(0)
 
@@ -168,28 +170,34 @@ def tile_attend_bucketbias_pl_kernel(tc, query, keys_words, keys_scales, bias, s
         probs = [sb.tile([P, I], F32, name=f"probs{h}", align_bytes=64)[:] for h in range(HALVES)]
         for h in range(HALVES):
             exponentiate(h)
-        vt_bf[0] = sb.tile([P, I], BF16, name="vt_bf0", tag="logits1", align_bytes=64)[:]
+        vt_early = sb.tile([P, 2 * I], BF16, name="vt_early", tag="logits1", align_bytes=64)
+        vt_bf[0] = vt_early[:, :I]
+        vt_bf[1] = vt_early[:, I:]
         turn_plane(0)
         gather_plane(1)
         w_all = sb.tile([P, HALVES * I], BF16, name="w_all", tag="plane1", align_bytes=64)
         w_bf = [w_all[:, h * I : (h + 1) * I] for h in range(HALVES)]
-        wt_bf = sb.tile([P, Q * PACK], BF16, name="wt_bf", align_bytes=64)
 
         def weigh(h):
             nc.vector.scalar_tensor_tensor(w_bf[h], probs[h], inv_sum[:, h : h + 1], size_rows[:], ALU.mult, ALU.mult)
+
+        def turn_weights(h, copy):
             words = w_bf[h].bitcast(F32)
-            turn_words([words[:, u * P : (u + 1) * P] for u in range(2)], wt_bf[:, h * P * PACK : (h + 1) * P * PACK], nc.scalar.copy)
+            turn_words([words[:, u * P : (u + 1) * P] for u in range(2)], wt_bf[:, h * P * PACK : (h + 1) * P * PACK], copy)
 
         turn_plane(1)
         weigh(0)
         weigh(1)
         gather_plane(2)
-        early_codes = sb.tile([P, Q + 2 * P], U32, name="early_codes", tag="plane2", align_bytes=64)
+        wt_bf = room2.tile([P, Q * PACK], BF16, name="wt_bf", offset=4096, align_bytes=64)
+        early_codes = room2.tile([P, Q + 2 * P], U32, name="early_codes", offset=0, align_bytes=64)
+        turn_weights(0, nc.vector.tensor_copy)
+        turn_weights(1, nc.scalar.copy)
+        turn_plane(2)
         w_codes = early_codes[:, :Q]
         v_codes[0] = early_codes[:, Q : Q + P]
         v_codes[1] = early_codes[:, Q + P :]
-        quantise_plane(0)
-        quantise_plane(1)
+        nc.vector.quantize_mx(out=early_codes[:, Q:].bitcast(FP8X4), scales=v_scales_all[:, : 2 * P], in_=vt_early[:])
         nc.vector.quantize_mx(out=w_codes.bitcast(FP8X4), scales=w_scales[:], in_=wt_bf[:])
 
         out_dealt = out_0.rearrange("(p r) q -> p r q", r=PACK)
@@ -200,7 +208,7 @@ def tile_attend_bucketbias_pl_kernel(tc, query, keys_words, keys_scales, bias, s
                 nc.tensor.matmul_mx(
                     out=acc[h][:, r, :],
                     lhsT=v_codes[r].bitcast(FP8X4),
-                    lhsT_scale=v_scales[r][:],
+                    lhsT_scale=v_scales[r],
                     rhs=w_codes[:, h * P : (h + 1) * P].bitcast(FP8X4),
                     rhs_scale=w_scales[:, h * P : (h + 1) * P],
                     start=True,
@@ -213,22 +221,20 @@ def tile_attend_bucketbias_pl_kernel(tc, query, keys_words, keys_scales, bias, s
         multiply(0)
         multiply(1)
         gather_plane(3)
-        behind_plane3 = sb.tile([P, PACK * Q + I // 2], F32, name="behind_plane3", tag="plane3", align_bytes=64)
-        y = behind_plane3[:, : PACK * Q].rearrange("p (r q) -> p r q", r=PACK)
-        vt_bf[2] = behind_plane3[:, PACK * Q :].bitcast(BF16)
-        for r in (2, 3):
-            v_codes[r] = sb.tile([P, P], U32, name=f"v_codes{r}", align_bytes=64)[:]
-        turn_plane(2)
+        y = room3.tile([P, PACK, Q], F32, name="y", offset=0, align_bytes=64)
+        late_codes = room3.tile([P, 2 * P], U32, name="late_codes", offset=4096, align_bytes=64)
+        v_codes[2] = late_codes[:, :P]
+        v_codes[3] = late_codes[:, P:]
         turn_plane(3)
+        quantise_plane(2)
         leave_bank(0, 0, 2, nc.vector.tensor_copy)
         leave_bank(1, 0, 2, nc.scalar.copy)
         nc.sync.dma_start(out_dealt[:, :2, :], y[:, :2, :])
-        quantise_plane(2)
         multiply(2)
-        quantise_plane(3)
-        for h in range(HALVES):
-            leave_bank(h, 2, 3, nc.scalar.copy)
+        leave_bank(0, 2, 3, nc.vector.tensor_copy)
+        leave_bank(1, 2, 3, nc.scalar.copy)
         nc.sync.dma_start(out_dealt[:, 2, :], y[:, 2, :])
+        quantise_plane(3)
         multiply(3)
 
         y_bf = [sb.tile([P, P, PACK], BF16, name=f"y_bf{h}", align_bytes=64) for h in range(HALVES)]
@@ -236,7 +242,8 @@ def tile_attend_bucketbias_pl_kernel(tc, query, keys_words, keys_scales, bias, s
         nc.scalar.copy(y_bf[1][:], acc[1][:].rearrange("p r q -> p q r"))
         leave_bank(0, 3, PACK, nc.vector.tensor_copy)
         leave_bank(1, 3, PACK, nc.scalar.copy)
-        nc.sync.dma_start(out_dealt[:, 3, :], y[:, 3, :])
+        for h in range(HALVES):
+            nc.sync.dma_start(out_dealt[:, 3, h * P : (h + 1) * P], y[:, 3, h * P : (h + 1) * P])
         y_codes = sb.tile([P, Q], U32, name="y_codes", align_bytes=64)
         y_scales = sb.tile([P, Q], U8, name="y_scales", align_bytes=64)
         for h in range(HALVES):

@@ -21,7 +21,7 @@ AX = mybir.AxisListType
 P = 128
 PACK = 4
 HALVES = Q // P
-LEAD = 768
+LEAD = 896
 VECTOR_SLOTS = (0, I, 320, 320)
 
 
@@ -46,18 +46,20 @@ def tile_attend_bucketbias_pl_kernel(tc, query, keys_words, keys_scales, bias, s
         kg_scales = sb.tile([P, I], U8, name="kg_scales", align_bytes=64)
         ident = sb.tile([P, P], F32, name="ident")
 
-        nc.gpsimd.memset(key_scales[:112, :].bitcast(I32), 0)
+        nc.vector.memset(key_scales[:, : T // 2].bitcast(I32), 0)
+        nc.gpsimd.memset(key_scales[:, T // 2 :].bitcast(I32), 0)
         nc.vector.memset(kg_scales[:].bitcast(I32), 0)
-        make_identity(nc, ident[:])
+        nc.vector.memset(ident[:], 0.0)
+        make_identity(nc, ident[:], nomemset=True)
 
         vals_dealt = vals.rearrange("(p r) t -> p r t", r=PACK)
         lead = room3.tile([P, LEAD], F32, name="lead", offset=0, align_bytes=64)
         size_col = sb.tile([P, PACK], F32, name="size_col")
-        nc.sync.dma_start(slot_tok[:], offs)
-        nc.sync.dma_start(key_scales[112:, :].bitcast(I32), keys_scales[0].bitcast(I32))
         nc.sync.dma_start(bias_sb[0][:], bias[:P, :])
+        nc.sync.dma_start(slot_tok[:], offs)
         nc.sync.dma_start(slot_bkt[:], offs2)
         nc.sync.dma_start(size_col[:], size.rearrange("o (p t) -> (o p) t", t=PACK))
+        nc.sync.dma_start(key_scales[32:96:4, :].bitcast(I32), keys_scales[0].bitcast(I32))
         nc.sync.dma_start(key_words[:].bitcast(I32), keys_words[0].bitcast(I32))
         nc.sync.dma_start(q_raw[:], query.rearrange("(p t) q -> p t q", t=PACK))
         nc.sync.dma_start(bias_sb[1][:], bias[P:, :])
@@ -66,7 +68,7 @@ def tile_attend_bucketbias_pl_kernel(tc, query, keys_words, keys_scales, bias, s
         kg_spread = sb.tile([P, I], U8, name="kg_spread", align_bytes=64)
         nc.vector.tensor_copy(kg_spread[:], key_scales[:].indirect(slot_tok[:]))
         for row in range(4):
-            nc.sync.dma_start(kg_scales[row:P:32, :].bitcast(I32), kg_spread[112 + row : P : 4, :].bitcast(I32))
+            nc.sync.dma_start(kg_scales[row:P:32, :].bitcast(I32), kg_spread[32 + 4 * row : 96 : 16, :].bitcast(I32))
         val_planes = [sb.tile([P, T], F32, name="val_plane0", tag="plane0", align_bytes=64)]
         nc.sync.dma_start(val_planes[0][:, LEAD:], vals_dealt[:, 0, LEAD:])
 

@@ -22,13 +22,14 @@ P = 128
 PACK = 4
 HALVES = Q // P
 LEAD = 896
-VECTOR_SLOTS = (0, I, 320, 320)
+VECTOR_SLOTS = (128, 384, 320, 320)
 
 
 def tile_attend_bucketbias_pl_kernel(tc, query, keys_words, keys_scales, bias, size, vals, offs, offs2, out_0, out_1, out_2):
     nc = tc.nc
     with ExitStack() as ctx:
         sb = ctx.enter_context(tc.tile_pool(name="sb", bufs=1))
+        room1 = ctx.enter_context(tc.tile_pool(name="room1", bufs=1))
         room2 = ctx.enter_context(tc.tile_pool(name="room2", bufs=1))
         room3 = ctx.enter_context(tc.tile_pool(name="room3", bufs=1))
         ps = ctx.enter_context(tc.psum_pool(name="ps", bufs=1))
@@ -41,7 +42,7 @@ def tile_attend_bucketbias_pl_kernel(tc, query, keys_words, keys_scales, bias, s
             sb.tile([P, U], F32, name="bias_sb0", align_bytes=64),
             sb.tile([P, U], F32, name="bias_sb1", align_bytes=64),
         ]
-        key_words = sb.tile([P, T], U16, name="key_words", tag="plane1", align_bytes=64)
+        key_words = room1.tile([P, T], U16, name="key_words", offset=0, align_bytes=64)
         q_raw = room2.tile([P, PACK, Q], F32, name="q_raw", offset=0, align_bytes=64)
         kg_scales = sb.tile([P, I], U8, name="kg_scales", align_bytes=64)
         ident = sb.tile([P, P], F32, name="ident")
@@ -59,7 +60,9 @@ def tile_attend_bucketbias_pl_kernel(tc, query, keys_words, keys_scales, bias, s
         nc.sync.dma_start(slot_tok[:], offs)
         nc.sync.dma_start(slot_bkt[:], offs2)
         nc.sync.dma_start(size_col[:], size.rearrange("o (p t) -> (o p) t", t=PACK))
-        nc.sync.dma_start(key_scales[32:96:4, :].bitcast(I32), keys_scales[0].bitcast(I32))
+        for c in range(2):
+            cols = slice(c * T // 2, (c + 1) * T // 2)
+            nc.sync.dma_start(key_scales[32:96:4, cols].bitcast(I32), keys_scales[0][:, cols].bitcast(I32))
         nc.sync.dma_start(key_words[:].bitcast(I32), keys_words[0].bitcast(I32))
         nc.sync.dma_start(q_raw[:], query.rearrange("(p t) q -> p t q", t=PACK))
         nc.sync.dma_start(bias_sb[1][:], bias[P:, :])
@@ -96,7 +99,7 @@ def tile_attend_bucketbias_pl_kernel(tc, query, keys_words, keys_scales, bias, s
         gather_bias(1)
         nc.vector.tensor_copy(val_planes[0][:, :LEAD], lead[:])
 
-        val_planes.append(sb.tile([P, T], F32, name="val_plane1", tag="plane1", align_bytes=64))
+        val_planes.append(room1.tile([P, T], F32, name="val_plane1", offset=0, align_bytes=64))
         val_planes.append(room2.tile([P, T], F32, name="val_plane2", offset=0, align_bytes=64))
         val_planes.append(room3.tile([P, T], F32, name="val_plane3", offset=0, align_bytes=64))
         for r in range(1, PACK):
@@ -128,12 +131,17 @@ def tile_attend_bucketbias_pl_kernel(tc, query, keys_words, keys_scales, bias, s
         vg_bf = [sb.tile([P, I], BF16, name=f"vg_bf{r}", align_bytes=64) for r in range(PACK)]
         vt_bf = {r: sb.tile([P, I], BF16, name=f"vt_bf{r}", align_bytes=64)[:] for r in (2, 3)}
 
-        def gather_plane(r):
+        def gather_on_vector(r):
             n = VECTOR_SLOTS[r]
-            if n > 0:
-                nc.vector.tensor_copy(vg_bf[r][:, :n], val_planes[r][:].indirect(slot_tok[:, : n // 16]))
-            if n < I:
-                nc.scalar.activation(vg_bf[r][:, n:], val_planes[r][:].indirect(slot_tok[:, n // 16 :]), ACT.Copy)
+            nc.vector.tensor_copy(vg_bf[r][:, :n], val_planes[r][:].indirect(slot_tok[:, : n // 16]))
+
+        def gather_on_scalar(r):
+            n = VECTOR_SLOTS[r]
+            nc.scalar.activation(vg_bf[r][:, n:], val_planes[r][:].indirect(slot_tok[:, n // 16 :]), ACT.Copy)
+
+        def gather_plane(r):
+            gather_on_vector(r)
+            gather_on_scalar(r)
 
         def turn_plane(r):
             words = vg_bf[r][:].bitcast(F32)
@@ -147,7 +155,7 @@ def tile_attend_bucketbias_pl_kernel(tc, query, keys_words, keys_scales, bias, s
         def quantise_plane(r):
             nc.vector.quantize_mx(out=v_codes[r].bitcast(FP8X4), scales=v_scales[r], in_=vt_bf[r])
 
-        gather_plane(0)
+        gather_on_scalar(0)
 
         logits = [sb.tile([P, I], F32, name=f"logits{h}", tag=f"logits{h}", align_bytes=64) for h in range(HALVES)]
         neg_max = [sb.tile([P, 1], F32, name=f"neg_max{h}") for h in range(HALVES)]
@@ -164,6 +172,7 @@ def tile_attend_bucketbias_pl_kernel(tc, query, keys_words, keys_scales, bias, s
             )
         for h in range(HALVES):
             nc.vector.tensor_reduce(neg_max[h][:], logits[h][:], AX.X, ALU.max, negate=True)
+        gather_on_vector(0)
 
         def exponentiate(h):
             nc.scalar.activation(probs[h], logits[h][:], ACT.Exp, bias=neg_max[h][:], accum_out=row_sum[:, h : h + 1])
@@ -172,12 +181,12 @@ def tile_attend_bucketbias_pl_kernel(tc, query, keys_words, keys_scales, bias, s
         probs = [sb.tile([P, I], F32, name=f"probs{h}", align_bytes=64)[:] for h in range(HALVES)]
         for h in range(HALVES):
             exponentiate(h)
-        vt_early = sb.tile([P, 2 * I], BF16, name="vt_early", tag="logits1", align_bytes=64)
+        gather_plane(1)
+        vt_early = room1.tile([P, 2 * I], BF16, name="vt_early", offset=4096, align_bytes=64)
         vt_bf[0] = vt_early[:, :I]
         vt_bf[1] = vt_early[:, I:]
         turn_plane(0)
-        gather_plane(1)
-        w_all = sb.tile([P, HALVES * I], BF16, name="w_all", tag="plane1", align_bytes=64)
+        w_all = room1.tile([P, HALVES * I], BF16, name="w_all", offset=0, align_bytes=64)
         w_bf = [w_all[:, h * I : (h + 1) * I] for h in range(HALVES)]
 
         def weigh(h):
@@ -233,10 +242,10 @@ def tile_attend_bucketbias_pl_kernel(tc, query, keys_words, keys_scales, bias, s
         leave_bank(1, 0, 2, nc.scalar.copy)
         nc.sync.dma_start(out_dealt[:, :2, :], y[:, :2, :])
         multiply(2)
-        leave_bank(0, 2, 3, nc.vector.tensor_copy)
-        leave_bank(1, 2, 3, nc.scalar.copy)
-        nc.sync.dma_start(out_dealt[:, 2, :], y[:, 2, :])
         quantise_plane(3)
+        for h in range(HALVES):
+            leave_bank(h, 2, 3, nc.scalar.copy)
+        nc.sync.dma_start(out_dealt[:, 2, :], y[:, 2, :])
         multiply(3)
 
         y_bf = [sb.tile([P, P, PACK], BF16, name=f"y_bf{h}", align_bytes=64) for h in range(HALVES)]

@@ -263,7 +263,7 @@ def tile_attend_bucketbias_pl_kernel(tc, query, keys_words, keys_scales, bias, s
             nc.sync.dma_start(out_1[0].rearrange("p c r -> p (c r)").bitcast(I32)[:, cols], y_codes[:, cols].bitcast(I32))
 
         for quad in range(4):
-            queue = nc.scalar if quad % 2 == 0 else nc.sync
+            queue = nc.scalar if quad == 0 else nc.sync
             queue.dma_start(
                 out_2[0][4 * quad : 4 * quad + 4, :].bitcast(I32),
                 y_scales[32 * quad : 32 * quad + 4, :].bitcast(I32),

@@ -105,7 +105,7 @@ def tile_attend_bucketbias_pl_kernel(tc, query, keys_words, keys_scales, bias, s
         for r in range(1, PACK):
             nc.sync.dma_start(val_planes[r][:], vals_dealt[:, r, :])
 
-        size_rows = ps.tile([P, I], F32, name="size_rows")
+        size_rows = ps.tile([P, I], F32, name="size_rows", tag="bank2")
         size_places = size_rows[:].rearrange("p (u c b) -> p u b c", u=2, b=2)
         for t in range(PACK):
             nc.tensor.transpose(size_places[:, t // 2, t % 2], size_col[:, t : t + 1].to_broadcast([P, P]), ident[:])
@@ -236,15 +236,38 @@ def tile_attend_bucketbias_pl_kernel(tc, query, keys_words, keys_scales, bias, s
         late_codes = room3.tile([P, 2 * P], U32, name="late_codes", offset=4096, align_bytes=64)
         v_codes[2] = late_codes[:, :P]
         v_codes[3] = late_codes[:, P:]
-        turn_plane(3)
+        words = vg_bf[3][:].bitcast(F32)
+        last_bank = turn.tile([P, 2, P], F32, name="turn_bank")
+        for u in range(2):
+            nc.tensor.transpose(last_bank[:, u, :], words[:, u::2], ident[:])
+        for c in range(2):
+            nc.scalar.copy(
+                vt_bf[3][:, c * I // 2 : (c + 1) * I // 2].bitcast(F32).rearrange("p (c u) -> p c u", u=2),
+                last_bank[:, :, c * P // 2 : (c + 1) * P // 2].rearrange("p u c -> p c u"),
+            )
         quantise_plane(2)
         leave_bank(0, 0, 2, nc.vector.tensor_copy)
         leave_bank(1, 0, 2, nc.scalar.copy)
         nc.sync.dma_start(out_dealt[:, :2, :], y[:, :2, :])
+        plane2_out = ps.tile([P, Q], F32, name="plane2_out", tag="bank2")
+        nc.tensor.matmul_mx(
+            out=plane2_out[:],
+            lhsT=v_codes[2].bitcast(FP8X4),
+            lhsT_scale=v_scales[2],
+            rhs=w_codes.bitcast(FP8X4),
+            rhs_scale=w_scales[:],
+            start=True,
+            stop=True,
+        )
         multiply(2)
-        quantise_plane(3)
-        for h in range(HALVES):
-            leave_bank(h, 2, 3, nc.scalar.copy)
+        for c in range(2):
+            cols = slice(c * P // 2, (c + 1) * P // 2)
+            nc.vector.quantize_mx(
+                out=v_codes[3][:, cols].bitcast(FP8X4),
+                scales=v_scales[3][:, cols],
+                in_=vt_bf[3][:, c * I // 2 : (c + 1) * I // 2],
+            )
+        nc.scalar.copy(y[:, 2, :], plane2_out[:])
         nc.sync.dma_start(out_dealt[:, 2, :], y[:, 2, :])
         multiply(3)
 
@@ -260,7 +283,7 @@ def tile_attend_bucketbias_pl_kernel(tc, query, keys_words, keys_scales, bias, s
         for h in range(HALVES):
             cols = slice(h * P, (h + 1) * P)
             nc.vector.quantize_mx(out=y_codes[:, cols].bitcast(FP8X4), scales=y_scales[:, cols], in_=y_bf[h][:].rearrange("p q r -> p (q r)"))
-            nc.sync.dma_start(out_1[0].rearrange("p c r -> p (c r)").bitcast(I32)[:, cols], y_codes[:, cols].bitcast(I32))
+        nc.sync.dma_start(out_1[0].rearrange("p c r -> p (c r)").bitcast(I32), y_codes[:].bitcast(I32))
 
         for quad in range(4):
             queue = nc.scalar if quad == 0 else nc.sync

@@ -60,9 +60,7 @@ def tile_attend_bucketbias_pl_kernel(tc, query, keys_words, keys_scales, bias, s
         nc.sync.dma_start(slot_tok[:], offs)
         nc.sync.dma_start(slot_bkt[:], offs2)
         nc.sync.dma_start(size_col[:], size.rearrange("o (p t) -> (o p) t", t=PACK))
-        for c in range(2):
-            cols = slice(c * T // 2, (c + 1) * T // 2)
-            nc.sync.dma_start(key_scales[32:96:4, cols].bitcast(I32), keys_scales[0][:, cols].bitcast(I32))
+        nc.sync.dma_start(key_scales[32:96:4, :].bitcast(I32), keys_scales[0].bitcast(I32))
         nc.sync.dma_start(key_words[:].bitcast(I32), keys_words[0].bitcast(I32))
         nc.sync.dma_start(q_raw[:], query.rearrange("(p t) q -> p t q", t=PACK))
         nc.sync.dma_start(bias_sb[1][:], bias[P:, :])
@@ -248,7 +246,6 @@ def tile_attend_bucketbias_pl_kernel(tc, query, keys_words, keys_scales, bias, s
         quantise_plane(2)
         leave_bank(0, 0, 2, nc.vector.tensor_copy)
         leave_bank(1, 0, 2, nc.scalar.copy)
-        nc.sync.dma_start(out_dealt[:, :2, :], y[:, :2, :])
         plane2_out = ps.tile([P, Q], F32, name="plane2_out", tag="bank2")
         nc.tensor.matmul_mx(
             out=plane2_out[:],
@@ -268,7 +265,7 @@ def tile_attend_bucketbias_pl_kernel(tc, query, keys_words, keys_scales, bias, s
                 in_=vt_bf[3][:, c * I // 2 : (c + 1) * I // 2],
             )
         nc.scalar.copy(y[:, 2, :], plane2_out[:])
-        nc.sync.dma_start(out_dealt[:, 2, :], y[:, 2, :])
+        nc.sync.dma_start(out_dealt[:, :3, :], y[:, :3, :])
         multiply(3)
 
         y_bf = [sb.tile([P, P, PACK], BF16, name=f"y_bf{h}", align_bytes=64) for h in range(HALVES)]
@@ -276,8 +273,7 @@ def tile_attend_bucketbias_pl_kernel(tc, query, keys_words, keys_scales, bias, s
         nc.scalar.copy(y_bf[1][:], acc[1][:].rearrange("p r q -> p q r"))
         leave_bank(0, 3, PACK, nc.vector.tensor_copy)
         leave_bank(1, 3, PACK, nc.scalar.copy)
-        for h in range(HALVES):
-            nc.sync.dma_start(out_dealt[:, 3, h * P : (h + 1) * P], y[:, 3, h * P : (h + 1) * P])
+        nc.sync.dma_start(out_dealt[:, 3, :], y[:, 3, :])
         y_codes = sb.tile([P, Q], U32, name="y_codes", align_bytes=64)
         y_scales = sb.tile([P, Q], U8, name="y_scales", align_bytes=64)
         for h in range(HALVES):

@@ -50,16 +50,17 @@ def tile_attend_bucketbias_pl_kernel(tc, query, keys_words, keys_scales, bias, s
         nc.vector.memset(key_scales[:, : T // 2].bitcast(I32), 0)
         nc.gpsimd.memset(key_scales[:, T // 2 :].bitcast(I32), 0)
         nc.vector.memset(kg_scales[:].bitcast(I32), 0)
+        size_in = sb.tile([P, P], F32, name="size_in")
+        nc.vector.memset(size_in[: P - PACK, :], 0.0)
         nc.vector.memset(ident[:], 0.0)
         make_identity(nc, ident[:], nomemset=True)
 
         vals_dealt = vals.rearrange("(p r) t -> p r t", r=PACK)
         lead = room3.tile([P, LEAD], F32, name="lead", offset=0, align_bytes=64)
-        size_col = sb.tile([P, PACK], F32, name="size_col")
         nc.sync.dma_start(bias_sb[0][:], bias[:P, :])
         nc.sync.dma_start(slot_tok[:], offs)
         nc.sync.dma_start(slot_bkt[:], offs2)
-        nc.sync.dma_start(size_col[:], size.rearrange("o (p t) -> (o p) t", t=PACK))
+        nc.sync.dma_start(size_in[P - PACK :, :], size.rearrange("o (r c) -> (o r) c", r=PACK))
         nc.sync.dma_start(key_scales[32:96:4, :].bitcast(I32), keys_scales[0].bitcast(I32))
         nc.sync.dma_start(key_words[:].bitcast(I32), keys_words[0].bitcast(I32))
         nc.sync.dma_start(q_raw[:], query.rearrange("(p t) q -> p t q", t=PACK))
@@ -103,10 +104,10 @@ def tile_attend_bucketbias_pl_kernel(tc, query, keys_words, keys_scales, bias, s
         for r in range(1, PACK):
             nc.sync.dma_start(val_planes[r][:], vals_dealt[:, r, :])
 
-        size_rows = ps.tile([P, I], F32, name="size_rows", tag="bank2")
-        size_places = size_rows[:].rearrange("p (u c b) -> p u b c", u=2, b=2)
-        for t in range(PACK):
-            nc.tensor.transpose(size_places[:, t // 2, t % 2], size_col[:, t : t + 1].to_broadcast([P, P]), ident[:])
+        size_turned = turn.tile([P, 2, P], F32, name="turn_bank")
+        nc.tensor.transpose(size_turned[:, 0, :], size_in[:], ident[:])
+        size_col = sb.tile([P, PACK], F32, name="size_col")
+        nc.scalar.copy(size_col[:], size_turned[:, 0, P - PACK :])
 
         scores = [ps.tile([P, I], F32, name=f"scores{h}", tag=f"bank{h}") for h in range(HALVES)]
         for h in range(HALVES):
@@ -168,6 +169,11 @@ def tile_attend_bucketbias_pl_kernel(tc, query, keys_words, keys_scales, bias, s
                 bias_g[h][:].rearrange("p (c u b) -> p u c b", u=2, b=2),
                 ALU.add,
             )
+        size_rows = ps.tile([P, I], F32, name="size_rows", tag="bank0")
+        size_places = size_rows[:].rearrange("p (u r j b) -> p r j u b", u=2, r=PACK, b=2)
+        for r in range(PACK):
+            nc.tensor.transpose(size_places[:, r], size_col[:, r : r + 1].to_broadcast([P, P]), ident[:])
+
         for h in range(HALVES):
             nc.vector.tensor_reduce(neg_max[h][:], logits[h][:], AX.X, ALU.max, negate=True)
         gather_on_vector(0)

@@ -274,17 +274,24 @@ def tile_attend_bucketbias_pl_kernel(tc, query, keys_words, keys_scales, bias, s
         nc.sync.dma_start(out_dealt[:, :3, :], y[:, :3, :])
         multiply(3)
 
-        y_bf = [sb.tile([P, P, PACK], BF16, name=f"y_bf{h}", align_bytes=64) for h in range(HALVES)]
-        nc.vector.tensor_copy(y_bf[0][:], acc[0][:].rearrange("p r q -> p q r"))
-        nc.scalar.copy(y_bf[1][:], acc[1][:].rearrange("p r q -> p q r"))
-        leave_bank(0, 3, PACK, nc.vector.tensor_copy)
-        leave_bank(1, 3, PACK, nc.scalar.copy)
-        nc.sync.dma_start(out_dealt[:, 3, :], y[:, 3, :])
+        y_bf = sb.tile([P, Q, PACK], BF16, name="y_bf", align_bytes=64)
         y_codes = sb.tile([P, Q], U32, name="y_codes", align_bytes=64)
         y_scales = sb.tile([P, Q], U8, name="y_scales", align_bytes=64)
-        for h in range(HALVES):
-            cols = slice(h * P, (h + 1) * P)
-            nc.vector.quantize_mx(out=y_codes[:, cols].bitcast(FP8X4), scales=y_scales[:, cols], in_=y_bf[h][:].rearrange("p q r -> p (q r)"))
+        nc.vector.tensor_copy(y_bf[:, :P, :], acc[0][:].rearrange("p r q -> p q r"))
+        leave_bank(1, 3, PACK, nc.scalar.copy)
+        for c in range(2):
+            nc.scalar.copy(
+                y_bf[:, P + c * P // 2 : P + (c + 1) * P // 2, :],
+                acc[1][:, :, c * P // 2 : (c + 1) * P // 2].rearrange("p r q -> p q r"),
+            )
+        leave_bank(0, 3, PACK, nc.vector.tensor_copy)
+        nc.sync.dma_start(out_dealt[:, 3, :], y[:, 3, :])
+        for first, end in ((0, P), (P, P + P // 2), (P + P // 2, Q)):
+            nc.vector.quantize_mx(
+                out=y_codes[:, first:end].bitcast(FP8X4),
+                scales=y_scales[:, first:end],
+                in_=y_bf[:, first:end, :].rearrange("p q r -> p (q r)"),
+            )
         nc.sync.dma_start(out_1[0].rearrange("p c r -> p (c r)").bitcast(I32), y_codes[:].bitcast(I32))
 
         for quad in range(4):

@@ -128,7 +128,7 @@ def tile_attend_bucketbias_pl_kernel(tc, query, keys_words, keys_scales, bias, s
             copy(dst_bf.bitcast(F32).rearrange("p (c u) -> p c u", u=2), bank[:].rearrange("p u c -> p c u"))
 
         vg_bf = [sb.tile([P, I], BF16, name=f"vg_bf{r}", align_bytes=64) for r in range(PACK)]
-        vt_bf = {r: sb.tile([P, I], BF16, name=f"vt_bf{r}", align_bytes=64)[:] for r in (2, 3)}
+        vt_bf = {r: sb.tile([P, I], BF16, name=f"vt_bf{r}", align_bytes=64)[:] for r in (3,)}
 
         def gather_on_vector(r):
             n = VECTOR_SLOTS[r]
@@ -208,7 +208,6 @@ def tile_attend_bucketbias_pl_kernel(tc, query, keys_words, keys_scales, bias, s
         early_codes = room2.tile([P, Q + 2 * P], U32, name="early_codes", offset=0, align_bytes=64)
         turn_weights(0, nc.vector.tensor_copy)
         turn_weights(1, nc.scalar.copy)
-        turn_plane(2)
         w_codes = early_codes[:, :Q]
         v_codes[0] = early_codes[:, Q : Q + P]
         v_codes[1] = early_codes[:, Q + P :]
@@ -240,6 +239,8 @@ def tile_attend_bucketbias_pl_kernel(tc, query, keys_words, keys_scales, bias, s
         late_codes = room3.tile([P, 2 * P], U32, name="late_codes", offset=4096, align_bytes=64)
         v_codes[2] = late_codes[:, :P]
         v_codes[3] = late_codes[:, P:]
+        vt_bf[2] = room3.tile([P, I], BF16, name="vt_bf2", offset=6144, align_bytes=64)[:]
+        turn_plane(2)
         words = vg_bf[3][:].bitcast(F32)
         last_bank = turn.tile([P, 2, P], F32, name="turn_bank")
         for u in range(2):
@@ -249,9 +250,9 @@ def tile_attend_bucketbias_pl_kernel(tc, query, keys_words, keys_scales, bias, s
                 vt_bf[3][:, c * I // 2 : (c + 1) * I // 2].bitcast(F32).rearrange("p (c u) -> p c u", u=2),
                 last_bank[:, :, c * P // 2 : (c + 1) * P // 2].rearrange("p u c -> p c u"),
             )
-        quantise_plane(2)
         leave_bank(0, 0, 2, nc.vector.tensor_copy)
         leave_bank(1, 0, 2, nc.scalar.copy)
+        quantise_plane(2)
         plane2_out = ps.tile([P, Q], F32, name="plane2_out", tag="bank2")
         nc.tensor.matmul_mx(
             out=plane2_out[:],

@@ -22,7 +22,7 @@ P = 128
 PACK = 4
 HALVES = Q // P
 LEAD = 896
-VECTOR_SLOTS = (128, 384, 320, 320)
+VECTOR_SLOTS = (128, 384, 320, 256)
 
 
 def tile_attend_bucketbias_pl_kernel(tc, query, keys_words, keys_scales, bias, size, vals, offs, offs2, out_0, out_1, out_2):

@@ -22,7 +22,7 @@ P = 128
 PACK = 4
 HALVES = Q // P
 LEAD = 896
-VECTOR_SLOTS = (128, 384, 320, 256)
+VECTOR_SLOTS = (0, 512, 256, 256)
 
 
 def tile_attend_bucketbias_pl_kernel(tc, query, keys_words, keys_scales, bias, size, vals, offs, offs2, out_0, out_1, out_2):
@@ -176,7 +176,6 @@ def tile_attend_bucketbias_pl_kernel(tc, query, keys_words, keys_scales, bias, s
 
         for h in range(HALVES):
             nc.vector.tensor_reduce(neg_max[h][:], logits[h][:], AX.X, ALU.max, negate=True)
-        gather_on_vector(0)
 
         def exponentiate(h):
             nc.scalar.activation(probs[h], logits[h][:], ACT.Exp, bias=neg_max[h][:], accum_out=row_sum[:, h : h + 1])
@@ -185,8 +184,8 @@ def tile_attend_bucketbias_pl_kernel(tc, query, keys_words, keys_scales, bias, s
         probs = [sb.tile([P, I], F32, name=f"probs{h}", align_bytes=64)[:] for h in range(HALVES)]
         for h in range(HALVES):
             exponentiate(h)
-        gather_plane(1)
-        vt_early = room1.tile([P, 2 * I], BF16, name="vt_early", offset=4096, align_bytes=64)
+        gather_on_vector(1)
+        vt_early = sb.tile([P, 2 * I], BF16, name="vt_early", tag="logits1", align_bytes=64)
         vt_bf[0] = vt_early[:, :I]
         vt_bf[1] = vt_early[:, I:]
         turn_plane(0)

@@ -22,7 +22,7 @@ P = 128
 PACK = 4
 HALVES = Q // P
 LEAD = 896
-VECTOR_SLOTS = (0, 512, 256, 256)
+VECTOR_SLOTS = (0, 448, 256, 288)
 
 
 def tile_attend_bucketbias_pl_kernel(tc, query, keys_words, keys_scales, bias, size, vals, offs, offs2, out_0, out_1, out_2):
@@ -33,7 +33,7 @@ def tile_attend_bucketbias_pl_kernel(tc, query, keys_words, keys_scales, bias, s
         room2 = ctx.enter_context(tc.tile_pool(name="room2", bufs=1))
         room3 = ctx.enter_context(tc.tile_pool(name="room3", bufs=1))
         ps = ctx.enter_context(tc.psum_pool(name="ps", bufs=1))
-        turn = ctx.enter_context(tc.psum_pool(name="turn", bufs=5))
+        turn = ctx.enter_context(tc.psum_pool(name="turn", bufs=4))
 
         slot_tok = sb.tile([P, I // 16], U16, name="slot_tok")
         slot_bkt = sb.tile([P, I // 16], U16, name="slot_bkt")
@@ -87,14 +87,20 @@ def tile_attend_bucketbias_pl_kernel(tc, query, keys_words, keys_scales, bias, s
         kg_words = sb.tile([P, I], U16, name="kg_words", align_bytes=64)
         nc.vector.tensor_copy(kg_words[:], key_words[:].indirect(slot_tok[:]))
 
-        q_bf = sb.tile([P, Q, PACK], BF16, name="q_bf", align_bytes=64)
-        nc.vector.tensor_copy(
-            q_bf[:].rearrange("p (c i) t -> p c t i", i=4),
-            q_raw[:].rearrange("p t (c i) -> p c t i", i=4),
-        )
+        q_bf = [sb.tile([P, P, PACK], BF16, name=f"q_bf{h}", align_bytes=64) for h in range(HALVES)]
         q_codes = sb.tile([P, Q], U32, name="q_codes", align_bytes=64)
         q_scales = sb.tile([P, Q], U8, name="q_scales", align_bytes=64)
-        nc.vector.quantize_mx(out=q_codes[:].bitcast(FP8X4), scales=q_scales[:], in_=q_bf[:].rearrange("p q t -> p (q t)"))
+        for h, copy in enumerate((nc.vector.tensor_copy, nc.scalar.copy)):
+            copy(
+                q_bf[h][:].rearrange("p (c i) t -> p c t i", i=4),
+                q_raw[:, :, h * P : (h + 1) * P].rearrange("p t (c i) -> p c t i", i=4),
+            )
+        for h in range(HALVES):
+            nc.vector.quantize_mx(
+                out=q_codes[:, h * P : (h + 1) * P].bitcast(FP8X4),
+                scales=q_scales[:, h * P : (h + 1) * P],
+                in_=q_bf[h][:].rearrange("p q t -> p (q t)"),
+            )
         gather_bias(1)
         nc.vector.tensor_copy(val_planes[0][:, :LEAD], lead[:])
 
@@ -109,14 +115,16 @@ def tile_attend_bucketbias_pl_kernel(tc, query, keys_words, keys_scales, bias, s
         size_col = sb.tile([P, PACK], F32, name="size_col")
         nc.scalar.copy(size_col[:], size_turned[:, 0, P - PACK :])
 
-        scores = [ps.tile([P, I], F32, name=f"scores{h}", tag=f"bank{h}") for h in range(HALVES)]
-        for h in range(HALVES):
+        pieces = ((0, 0, I // 2, "bank0"), (0, I // 2, I, "bank3"), (1, 0, I // 2, "bank1"), (1, I // 2, I, "bank2"))
+        scores = []
+        for h, first, end, bank in pieces:
+            scores.append(ps.tile([P, end - first], F32, name=f"scores{h}_{first}", tag=bank))
             nc.tensor.matmul_mx(
-                out=scores[h][:],
+                out=scores[-1][:],
                 lhsT=q_codes[:, h * P : (h + 1) * P].bitcast(FP8X4),
                 lhsT_scale=q_scales[:, h * P : (h + 1) * P],
-                rhs=kg_words[:].bitcast(FP4X4),
-                rhs_scale=kg_scales[:],
+                rhs=kg_words[:, first:end].bitcast(FP4X4),
+                rhs_scale=kg_scales[:, first:end],
                 start=True,
                 stop=True,
             )
@@ -162,11 +170,11 @@ def tile_attend_bucketbias_pl_kernel(tc, query, keys_words, keys_scales, bias, s
         inv_sum = sb.tile([P, HALVES], F32, name="inv_sum")
         minus_one = sb.tile([P, 1], F32, name="minus_one")
         nc.gpsimd.memset(minus_one[:], -1.0)
-        for h in range(HALVES):
+        for (h, first, end, bank), piece in zip(pieces, scores):
             nc.vector.tensor_tensor(
-                logits[h][:].rearrange("p (u c b) -> p u c b", u=2, b=2),
-                scores[h][:].rearrange("p (c u b) -> p u c b", u=2, b=2),
-                bias_g[h][:].rearrange("p (c u b) -> p u c b", u=2, b=2),
+                logits[h][:].rearrange("p (u c b) -> p u c b", u=2, b=2)[:, :, first // 4 : end // 4, :],
+                piece[:].rearrange("p (c u b) -> p u c b", u=2, b=2),
+                bias_g[h][:, first:end].rearrange("p (c u b) -> p u c b", u=2, b=2),
                 ALU.add,
             )
         size_rows = ps.tile([P, I], F32, name="size_rows", tag="bank0")
@@ -184,10 +192,8 @@ def tile_attend_bucketbias_pl_kernel(tc, query, keys_words, keys_scales, bias, s
         probs = [sb.tile([P, I], F32, name=f"probs{h}", align_bytes=64)[:] for h in range(HALVES)]
         for h in range(HALVES):
             exponentiate(h)
-        gather_on_vector(1)
-        vt_early = sb.tile([P, 2 * I], BF16, name="vt_early", tag="logits1", align_bytes=64)
-        vt_bf[0] = vt_early[:, :I]
-        vt_bf[1] = vt_early[:, I:]
+        gather_plane(1)
+        vt_bf[0] = room1.tile([P, I], BF16, name="vt_bf0", offset=4096, align_bytes=64)[:]
         turn_plane(0)
         w_all = room1.tile([P, HALVES * I], BF16, name="w_all", offset=0, align_bytes=64)
         w_bf = [w_all[:, h * I : (h + 1) * I] for h in range(HALVES)]
@@ -199,19 +205,31 @@ def tile_attend_bucketbias_pl_kernel(tc, query, keys_words, keys_scales, bias, s
             words = w_bf[h].bitcast(F32)
             turn_words([words[:, u * P : (u + 1) * P] for u in range(2)], wt_bf[:, h * P * PACK : (h + 1) * P * PACK], copy)
 
-        turn_plane(1)
+        def quantise_weights(h):
+            nc.vector.quantize_mx(
+                out=w_codes[:, h * P : (h + 1) * P].bitcast(FP8X4),
+                scales=w_scales[:, h * P : (h + 1) * P],
+                in_=wt_bf[:, h * P * PACK : (h + 1) * P * PACK],
+            )
+
         weigh(0)
         weigh(1)
         gather_plane(2)
-        wt_bf = room2.tile([P, Q * PACK], BF16, name="wt_bf", offset=4096, align_bytes=64)
         early_codes = room2.tile([P, Q + 2 * P], U32, name="early_codes", offset=0, align_bytes=64)
-        turn_weights(0, nc.vector.tensor_copy)
-        turn_weights(1, nc.scalar.copy)
+        wt_bf = room2.tile([P, Q * PACK], BF16, name="wt_bf", offset=4096, align_bytes=64)
+        vt_bf[1] = room2.tile([P, I], BF16, name="vt_bf1", offset=6144, align_bytes=64)[:]
+        vt_bf[2] = sb.tile([P, I], BF16, name="vt_bf2", align_bytes=64)[:]
         w_codes = early_codes[:, :Q]
         v_codes[0] = early_codes[:, Q : Q + P]
         v_codes[1] = early_codes[:, Q + P :]
-        nc.vector.quantize_mx(out=early_codes[:, Q:].bitcast(FP8X4), scales=v_scales_all[:, : 2 * P], in_=vt_early[:])
-        nc.vector.quantize_mx(out=w_codes.bitcast(FP8X4), scales=w_scales[:], in_=wt_bf[:])
+        quantise_plane(0)
+        turn_weights(0, nc.vector.tensor_copy)
+        turn_weights(1, nc.scalar.copy)
+        turn_plane(1)
+        quantise_weights(1)
+        quantise_weights(0)
+        quantise_plane(1)
+        turn_plane(2)
 
         out_dealt = out_0.rearrange("(p r) q -> p r q", r=PACK)
         acc = [ps.tile([P, PACK, P], F32, name=f"acc{h}", tag=f"bank{h}") for h in range(HALVES)]
@@ -238,8 +256,6 @@ def tile_attend_bucketbias_pl_kernel(tc, query, keys_words, keys_scales, bias, s
         late_codes = room3.tile([P, 2 * P], U32, name="late_codes", offset=4096, align_bytes=64)
         v_codes[2] = late_codes[:, :P]
         v_codes[3] = late_codes[:, P:]
-        vt_bf[2] = room3.tile([P, I], BF16, name="vt_bf2", offset=6144, align_bytes=64)[:]
-        turn_plane(2)
         words = vg_bf[3][:].bitcast(F32)
         last_bank = turn.tile([P, 2, P], F32, name="turn_bank")
         for u in range(2):

@@ -49,6 +49,10 @@ def tile_attend_bucketbias_pl_kernel(tc, query, keys_words, keys_scales, bias, s
 
         nc.vector.memset(key_scales[:, : T // 2].bitcast(I32), 0)
         nc.gpsimd.memset(key_scales[:, T // 2 :].bitcast(I32), 0)
+        zero = sb.tile([P, 1], F32, name="zero")
+        minus_one = sb.tile([P, 1], F32, name="minus_one")
+        nc.vector.memset(zero[:], 0.0)
+        nc.scalar.activation(minus_one[:], zero[:], ACT.Copy, bias=-1.0)
         nc.vector.memset(kg_scales[:].bitcast(I32), 0)
         size_in = sb.tile([P, P], F32, name="size_in")
         nc.vector.memset(size_in[: P - PACK, :], 0.0)
@@ -168,8 +172,6 @@ def tile_attend_bucketbias_pl_kernel(tc, query, keys_words, keys_scales, bias, s
         neg_max = [sb.tile([P, 1], F32, name=f"neg_max{h}") for h in range(HALVES)]
         row_sum = sb.tile([P, HALVES], F32, name="row_sum")
         inv_sum = sb.tile([P, HALVES], F32, name="inv_sum")
-        minus_one = sb.tile([P, 1], F32, name="minus_one")
-        nc.gpsimd.memset(minus_one[:], -1.0)
         for (h, first, end, bank), piece in zip(pieces, scores):
             nc.vector.tensor_tensor(
                 logits[h][:].rearrange("p (u c b) -> p u c b", u=2, b=2)[:, :, first // 4 : end // 4, :],
@@ -224,11 +226,11 @@ def tile_attend_bucketbias_pl_kernel(tc, query, keys_words, keys_scales, bias, s
         v_codes[1] = early_codes[:, Q + P :]
         quantise_plane(0)
         turn_weights(0, nc.vector.tensor_copy)
-        turn_weights(1, nc.scalar.copy)
         turn_plane(1)
-        quantise_weights(1)
-        quantise_weights(0)
+        turn_weights(1, nc.scalar.copy)
         quantise_plane(1)
+        quantise_weights(0)
+        quantise_weights(1)
         turn_plane(2)
 
         out_dealt = out_0.rearrange("(p r) q -> p r q", r=PACK)

@@ -22,7 +22,7 @@ P = 128
 PACK = 4
 HALVES = Q // P
 LEAD = 896
-VECTOR_SLOTS = (0, 448, 256, 288)
+VECTOR_SLOTS = (0, 448, 224, 288)
 
 
 def tile_attend_bucketbias_pl_kernel(tc, query, keys_words, keys_scales, bias, size, vals, offs, offs2, out_0, out_1, out_2):
@@ -91,20 +91,14 @@ def tile_attend_bucketbias_pl_kernel(tc, query, keys_words, keys_scales, bias, s
         kg_words = sb.tile([P, I], U16, name="kg_words", align_bytes=64)
         nc.vector.tensor_copy(kg_words[:], key_words[:].indirect(slot_tok[:]))
 
-        q_bf = [sb.tile([P, P, PACK], BF16, name=f"q_bf{h}", align_bytes=64) for h in range(HALVES)]
+        q_bf = sb.tile([P, Q, PACK], BF16, name="q_bf", align_bytes=64)
+        nc.vector.tensor_copy(
+            q_bf[:].rearrange("p (c i) t -> p c t i", i=4),
+            q_raw[:].rearrange("p t (c i) -> p c t i", i=4),
+        )
         q_codes = sb.tile([P, Q], U32, name="q_codes", align_bytes=64)
         q_scales = sb.tile([P, Q], U8, name="q_scales", align_bytes=64)
-        for h, copy in enumerate((nc.vector.tensor_copy, nc.scalar.copy)):
-            copy(
-                q_bf[h][:].rearrange("p (c i) t -> p c t i", i=4),
-                q_raw[:, :, h * P : (h + 1) * P].rearrange("p t (c i) -> p c t i", i=4),
-            )
-        for h in range(HALVES):
-            nc.vector.quantize_mx(
-                out=q_codes[:, h * P : (h + 1) * P].bitcast(FP8X4),
-                scales=q_scales[:, h * P : (h + 1) * P],
-                in_=q_bf[h][:].rearrange("p q t -> p (q t)"),
-            )
+        nc.vector.quantize_mx(out=q_codes[:].bitcast(FP8X4), scales=q_scales[:], in_=q_bf[:].rearrange("p q t -> p (q t)"))
         gather_bias(1)
         nc.vector.tensor_copy(val_planes[0][:, :LEAD], lead[:])
 

@@ -37,14 +37,14 @@ def tile_attend_bucketbias_pl_kernel(tc, query, keys_words, keys_scales, bias, s
 
         slot_tok = sb.tile([P, I // 16], U16, name="slot_tok")
         slot_bkt = sb.tile([P, I // 16], U16, name="slot_bkt")
-        key_scales = sb.tile([P, T], U8, name="key_scales", tag="plane0", align_bytes=64)
+        key_scales = sb.tile([P, T], U8, name="key_scales", tag="plane0", align_bytes=256)
         bias_sb = [
-            sb.tile([P, U], F32, name="bias_sb0", align_bytes=64),
-            sb.tile([P, U], F32, name="bias_sb1", align_bytes=64),
+            sb.tile([P, U], F32, name="bias_sb0", align_bytes=256),
+            sb.tile([P, U], F32, name="bias_sb1", align_bytes=256),
         ]
-        key_words = room1.tile([P, T], U16, name="key_words", offset=0, align_bytes=64)
-        q_raw = room2.tile([P, PACK, Q], F32, name="q_raw", offset=0, align_bytes=64)
-        kg_scales = sb.tile([P, I], U8, name="kg_scales", align_bytes=64)
+        key_words = room1.tile([P, T], U16, name="key_words", offset=0, align_bytes=256)
+        q_raw = room2.tile([P, PACK, Q], F32, name="q_raw", offset=0, align_bytes=256)
+        kg_scales = sb.tile([P, I], U8, name="kg_scales", align_bytes=256)
         ident = sb.tile([P, P], F32, name="ident")
 
         nc.vector.memset(key_scales[:, : T // 2].bitcast(I32), 0)
@@ -54,13 +54,13 @@ def tile_attend_bucketbias_pl_kernel(tc, query, keys_words, keys_scales, bias, s
         nc.vector.memset(zero[:], 0.0)
         nc.scalar.activation(minus_one[:], zero[:], ACT.Copy, bias=-1.0)
         nc.vector.memset(kg_scales[:].bitcast(I32), 0)
-        size_in = sb.tile([P, P], F32, name="size_in")
+        size_in = sb.tile([P, P], F32, name="size_in", align_bytes=256)
         nc.vector.memset(size_in[: P - PACK, :], 0.0)
         nc.vector.memset(ident[:], 0.0)
         make_identity(nc, ident[:], nomemset=True)
 
         vals_dealt = vals.rearrange("(p r) t -> p r t", r=PACK)
-        lead = room3.tile([P, LEAD], F32, name="lead", offset=0, align_bytes=64)
+        lead = room3.tile([P, LEAD], F32, name="lead", offset=0, align_bytes=256)
         nc.sync.dma_start(bias_sb[0][:], bias[:P, :])
         nc.sync.dma_start(slot_tok[:], offs)
         nc.sync.dma_start(slot_bkt[:], offs2)
@@ -71,11 +71,11 @@ def tile_attend_bucketbias_pl_kernel(tc, query, keys_words, keys_scales, bias, s
         nc.sync.dma_start(bias_sb[1][:], bias[P:, :])
         nc.sync.dma_start(lead[:], vals_dealt[:, 0, :LEAD])
 
-        kg_spread = sb.tile([P, I], U8, name="kg_spread", align_bytes=64)
+        kg_spread = sb.tile([P, I], U8, name="kg_spread", align_bytes=256)
         nc.vector.tensor_copy(kg_spread[:], key_scales[:].indirect(slot_tok[:]))
         for row in range(4):
             nc.sync.dma_start(kg_scales[row:P:32, :].bitcast(I32), kg_spread[32 + 4 * row : 96 : 16, :].bitcast(I32))
-        val_planes = [sb.tile([P, T], F32, name="val_plane0", tag="plane0", align_bytes=64)]
+        val_planes = [sb.tile([P, T], F32, name="val_plane0", tag="plane0", align_bytes=256)]
         nc.sync.dma_start(val_planes[0][:, LEAD:], vals_dealt[:, 0, LEAD:])
 
         bias_g = [sb.tile([P, I], F32, name=f"bias_g{h}", align_bytes=64) for h in range(HALVES)]
@@ -102,9 +102,9 @@ def tile_attend_bucketbias_pl_kernel(tc, query, keys_words, keys_scales, bias, s
         gather_bias(1)
         nc.vector.tensor_copy(val_planes[0][:, :LEAD], lead[:])
 
-        val_planes.append(room1.tile([P, T], F32, name="val_plane1", offset=0, align_bytes=64))
-        val_planes.append(room2.tile([P, T], F32, name="val_plane2", offset=0, align_bytes=64))
-        val_planes.append(room3.tile([P, T], F32, name="val_plane3", offset=0, align_bytes=64))
+        val_planes.append(room1.tile([P, T], F32, name="val_plane1", offset=0, align_bytes=256))
+        val_planes.append(room2.tile([P, T], F32, name="val_plane2", offset=0, align_bytes=256))
+        val_planes.append(room3.tile([P, T], F32, name="val_plane3", offset=0, align_bytes=256))
         for r in range(1, PACK):
             nc.sync.dma_start(val_planes[r][:], vals_dealt[:, r, :])
 
@@ -189,9 +189,9 @@ def tile_attend_bucketbias_pl_kernel(tc, query, keys_words, keys_scales, bias, s
         for h in range(HALVES):
             exponentiate(h)
         gather_plane(1)
-        vt_bf[0] = room1.tile([P, I], BF16, name="vt_bf0", offset=4096, align_bytes=64)[:]
+        vt_bf[0] = room1.tile([P, I], BF16, name="vt_bf0", offset=4096, align_bytes=256)[:]
         turn_plane(0)
-        w_all = room1.tile([P, HALVES * I], BF16, name="w_all", offset=0, align_bytes=64)
+        w_all = room1.tile([P, HALVES * I], BF16, name="w_all", offset=0, align_bytes=256)
         w_bf = [w_all[:, h * I : (h + 1) * I] for h in range(HALVES)]
 
         def weigh(h):
@@ -211,9 +211,9 @@ def tile_attend_bucketbias_pl_kernel(tc, query, keys_words, keys_scales, bias, s
         weigh(0)
         weigh(1)
         gather_plane(2)
-        early_codes = room2.tile([P, Q + 2 * P], U32, name="early_codes", offset=0, align_bytes=64)
-        wt_bf = room2.tile([P, Q * PACK], BF16, name="wt_bf", offset=4096, align_bytes=64)
-        vt_bf[1] = room2.tile([P, I], BF16, name="vt_bf1", offset=6144, align_bytes=64)[:]
+        early_codes = room2.tile([P, Q + 2 * P], U32, name="early_codes", offset=0, align_bytes=256)
+        wt_bf = room2.tile([P, Q * PACK], BF16, name="wt_bf", offset=4096, align_bytes=256)
+        vt_bf[1] = room2.tile([P, I], BF16, name="vt_bf1", offset=6144, align_bytes=256)[:]
         vt_bf[2] = sb.tile([P, I], BF16, name="vt_bf2", align_bytes=64)[:]
         w_codes = early_codes[:, :Q]
         v_codes[0] = early_codes[:, Q : Q + P]
@@ -248,8 +248,8 @@ def tile_attend_bucketbias_pl_kernel(tc, query, keys_words, keys_scales, bias, s
         multiply(0)
         multiply(1)
         gather_plane(3)
-        y = room3.tile([P, PACK, Q], F32, name="y", offset=0, align_bytes=64)
-        late_codes = room3.tile([P, 2 * P], U32, name="late_codes", offset=4096, align_bytes=64)
+        y = room3.tile([P, PACK, Q], F32, name="y", offset=0, align_bytes=256)
+        late_codes = room3.tile([P, 2 * P], U32, name="late_codes", offset=4096, align_bytes=256)
         v_codes[2] = late_codes[:, :P]
         v_codes[3] = late_codes[:, P:]
         words = vg_bf[3][:].bitcast(F32)
@@ -287,8 +287,8 @@ def tile_attend_bucketbias_pl_kernel(tc, query, keys_words, keys_scales, bias, s
         multiply(3)
 
         y_bf = sb.tile([P, Q, PACK], BF16, name="y_bf", align_bytes=64)
-        y_codes = sb.tile([P, Q], U32, name="y_codes", align_bytes=64)
-        y_scales = sb.tile([P, Q], U8, name="y_scales", align_bytes=64)
+        y_codes = sb.tile([P, Q], U32, name="y_codes", align_bytes=256)
+        y_scales = sb.tile([P, Q], U8, name="y_scales", align_bytes=256)
         nc.vector.tensor_copy(y_bf[:, :P, :], acc[0][:].rearrange("p r q -> p q r"))
         leave_bank(1, 3, PACK, nc.scalar.copy)
         for c in range(2):

from contextlib import ExitStack

import concourse.mybir as mybir
from concourse.masks import make_identity

D, T, I, Q, E, U = 512, 2048, 512, 256, 512, 512
FLOPS = 2 * D * Q * I + 2 * I * E * Q

F32 = mybir.dt.float32
BF16 = mybir.dt.bfloat16
I32 = mybir.dt.int32
U32 = mybir.dt.uint32
U16 = mybir.dt.uint16
U8 = mybir.dt.uint8
FP8X4 = mybir.dt.float8_e4m3fn_x4
FP4X4 = mybir.dt.float4_e2m1fn_x4
ALU = mybir.AluOpType
ACT = mybir.ActivationFunctionType
AX = mybir.AxisListType

P = 128
PACK = 4
HALVES = Q // P
LEAD = 896
VECTOR_SLOTS = (0, 448, 224, 288)


def tile_attend_bucketbias_pl_kernel(tc, query, keys_words, keys_scales, bias, size, vals, offs, offs2, out_0, out_1, out_2):
    nc = tc.nc
    with ExitStack() as ctx:
        sb = ctx.enter_context(tc.tile_pool(name="sb", bufs=1))
        room1 = ctx.enter_context(tc.tile_pool(name="room1", bufs=1))
        room2 = ctx.enter_context(tc.tile_pool(name="room2", bufs=1))
        room3 = ctx.enter_context(tc.tile_pool(name="room3", bufs=1))
        ps = ctx.enter_context(tc.psum_pool(name="ps", bufs=1))
        turn = ctx.enter_context(tc.psum_pool(name="turn", bufs=4))

        slot_tok = sb.tile([P, I // 16], U16, name="slot_tok")
        slot_bkt = sb.tile([P, I // 16], U16, name="slot_bkt")
        key_scales = sb.tile([P, T], U8, name="key_scales", tag="plane0", align_bytes=256)
        bias_sb = [
            sb.tile([P, U], F32, name="bias_sb0", align_bytes=256),
            sb.tile([P, U], F32, name="bias_sb1", align_bytes=256),
        ]
        key_words = room1.tile([P, T], U16, name="key_words", offset=0, align_bytes=256)
        q_raw = room2.tile([P, PACK, Q], F32, name="q_raw", offset=0, align_bytes=256)
        kg_scales = sb.tile([P, I], U8, name="kg_scales", align_bytes=256)
        ident = sb.tile([P, P], F32, name="ident")

        nc.vector.memset(key_scales[:, : T // 2].bitcast(I32), 0)
        nc.gpsimd.memset(key_scales[:, T // 2 :].bitcast(I32), 0)
        zero = sb.tile([P, 1], F32, name="zero")
        minus_one = sb.tile([P, 1], F32, name="minus_one")
        nc.vector.memset(zero[:], 0.0)
        nc.scalar.activation(minus_one[:], zero[:], ACT.Copy, bias=-1.0)
        nc.vector.memset(kg_scales[:].bitcast(I32), 0)
        size_in = sb.tile([P, P], F32, name="size_in", align_bytes=256)
        nc.vector.memset(size_in[: P - PACK, :], 0.0)
        nc.vector.memset(ident[:], 0.0)
        make_identity(nc, ident[:], nomemset=True)

        vals_dealt = vals.rearrange("(p r) t -> p r t", r=PACK)
        lead = room3.tile([P, LEAD], F32, name="lead", offset=0, align_bytes=256)
        nc.sync.dma_start(bias_sb[0][:], bias[:P, :])
        nc.sync.dma_start(slot_tok[:], offs)
        nc.sync.dma_start(slot_bkt[:], offs2)
        nc.sync.dma_start(size_in[P - PACK :, :], size.rearrange("o (r c) -> (o r) c", r=PACK))
        nc.sync.dma_start(key_scales[32:96:4, :].bitcast(I32), keys_scales[0].bitcast(I32))
        nc.sync.dma_start(key_words[:].bitcast(I32), keys_words[0].bitcast(I32))
        nc.sync.dma_start(q_raw[:], query.rearrange("(p t) q -> p t q", t=PACK))
        nc.sync.dma_start(bias_sb[1][:], bias[P:, :])
        nc.sync.dma_start(lead[:], vals_dealt[:, 0, :LEAD])

        kg_spread = sb.tile([P, I], U8, name="kg_spread", align_bytes=256)
        nc.vector.tensor_copy(kg_spread[:], key_scales[:].indirect(slot_tok[:]))
        for row in range(4):
            nc.sync.dma_start(kg_scales[row:P:32, :].bitcast(I32), kg_spread[32 + 4 * row : 96 : 16, :].bitcast(I32))
        val_planes = [sb.tile([P, T], F32, name="val_plane0", tag="plane0", align_bytes=256)]
        nc.sync.dma_start(val_planes[0][:, LEAD:], vals_dealt[:, 0, LEAD:])

        bias_g = [sb.tile([P, I], F32, name=f"bias_g{h}", align_bytes=64) for h in range(HALVES)]

        def gather_bias(h):
            n = I // 2
            for c in range(2):
                offsets = slot_bkt[:, c * n // 16 : (c + 1) * n // 16]
                nc.scalar.activation(bias_g[h][:, c * n : (c + 1) * n], bias_sb[h][:].indirect(offsets), ACT.Copy)

        gather_bias(0)

        kg_words = sb.tile([P, I], U16, name="kg_words", align_bytes=64)
        nc.vector.tensor_copy(kg_words[:], key_words[:].indirect(slot_tok[:]))

        q_bf = sb.tile([P, Q, PACK], BF16, name="q_bf", align_bytes=64)
        nc.vector.tensor_copy(
            q_bf[:].rearrange("p (c i) t -> p c t i", i=4),
            q_raw[:].rearrange("p t (c i) -> p c t i", i=4),
        )
        q_codes = sb.tile([P, Q], U32, name="q_codes", align_bytes=64)
        q_scales = sb.tile([P, Q], U8, name="q_scales", align_bytes=64)
        nc.vector.quantize_mx(out=q_codes[:].bitcast(FP8X4), scales=q_scales[:], in_=q_bf[:].rearrange("p q t -> p (q t)"))
        gather_bias(1)
        nc.vector.tensor_copy(val_planes[0][:, :LEAD], lead[:])

        val_planes.append(room1.tile([P, T], F32, name="val_plane1", offset=0, align_bytes=256))
        val_planes.append(room2.tile([P, T], F32, name="val_plane2", offset=0, align_bytes=256))
        val_planes.append(room3.tile([P, T], F32, name="val_plane3", offset=0, align_bytes=256))
        for r in range(1, PACK):
            nc.sync.dma_start(val_planes[r][:], vals_dealt[:, r, :])

        size_turned = turn.tile([P, 2, P], F32, name="turn_bank")
        nc.tensor.transpose(size_turned[:, 0, :], size_in[:], ident[:])
        size_col = sb.tile([P, PACK], F32, name="size_col")
        nc.scalar.copy(size_col[:], size_turned[:, 0, P - PACK :])

        pieces = ((0, 0, I // 2, "bank0"), (0, I // 2, I, "bank3"), (1, 0, I // 2, "bank1"), (1, I // 2, I, "bank2"))
        scores = []
        for h, first, end, bank in pieces:
            scores.append(ps.tile([P, end - first], F32, name=f"scores{h}_{first}", tag=bank))
            nc.tensor.matmul_mx(
                out=scores[-1][:],
                lhsT=q_codes[:, h * P : (h + 1) * P].bitcast(FP8X4),
                lhsT_scale=q_scales[:, h * P : (h + 1) * P],
                rhs=kg_words[:, first:end].bitcast(FP4X4),
                rhs_scale=kg_scales[:, first:end],
                start=True,
                stop=True,
            )

        def turn_words(word_sets, dst_bf, copy):
            bank = turn.tile([P, 2, P], F32, name="turn_bank")
            for u in range(2):
                nc.tensor.transpose(bank[:, u, :], word_sets[u], ident[:])
            copy(dst_bf.bitcast(F32).rearrange("p (c u) -> p c u", u=2), bank[:].rearrange("p u c -> p c u"))

        vg_bf = [sb.tile([P, I], BF16, name=f"vg_bf{r}", align_bytes=64) for r in range(PACK)]
        vt_bf = {r: sb.tile([P, I], BF16, name=f"vt_bf{r}", align_bytes=64)[:] for r in (3,)}

        def gather_on_vector(r):
            n = VECTOR_SLOTS[r]
            nc.vector.tensor_copy(vg_bf[r][:, :n], val_planes[r][:].indirect(slot_tok[:, : n // 16]))

        def gather_on_scalar(r):
            n = VECTOR_SLOTS[r]
            nc.scalar.activation(vg_bf[r][:, n:], val_planes[r][:].indirect(slot_tok[:, n // 16 :]), ACT.Copy)

        def gather_plane(r):
            gather_on_vector(r)
            gather_on_scalar(r)

        def turn_plane(r):
            words = vg_bf[r][:].bitcast(F32)
            turn_words([words[:, u::2] for u in range(2)], vt_bf[r], nc.scalar.copy)

        v_codes = {}
        v_scales_all = sb.tile([P, PACK * P], U8, name="v_scales", align_bytes=64)
        v_scales = [v_scales_all[:, r * P : (r + 1) * P] for r in range(PACK)]
        w_scales = sb.tile([P, Q], U8, name="w_scales", align_bytes=64)

        def quantise_plane(r):
            nc.vector.quantize_mx(out=v_codes[r].bitcast(FP8X4), scales=v_scales[r], in_=vt_bf[r])

        gather_on_scalar(0)

        logits = [sb.tile([P, I], F32, name=f"logits{h}", tag=f"logits{h}", align_bytes=64) for h in range(HALVES)]
        neg_max = [sb.tile([P, 1], F32, name=f"neg_max{h}") for h in range(HALVES)]
        row_sum = sb.tile([P, HALVES], F32, name="row_sum")
        inv_sum = sb.tile([P, HALVES], F32, name="inv_sum")
        for (h, first, end, bank), piece in zip(pieces, scores):
            nc.vector.tensor_tensor(
                logits[h][:].rearrange("p (u c b) -> p u c b", u=2, b=2)[:, :, first // 4 : end // 4, :],
                piece[:].rearrange("p (c u b) -> p u c b", u=2, b=2),
                bias_g[h][:, first:end].rearrange("p (c u b) -> p u c b", u=2, b=2),
                ALU.add,
            )
        size_rows = ps.tile([P, I], F32, name="size_rows", tag="bank0")
        size_places = size_rows[:].rearrange("p (u r j b) -> p r j u b", u=2, r=PACK, b=2)
        for r in range(PACK):
            nc.tensor.transpose(size_places[:, r], size_col[:, r : r + 1].to_broadcast([P, P]), ident[:])

        for h in range(HALVES):
            nc.vector.tensor_reduce(neg_max[h][:], logits[h][:], AX.X, ALU.max, negate=True)

        def exponentiate(h):
            nc.scalar.activation(probs[h], logits[h][:], ACT.Exp, bias=neg_max[h][:], accum_out=row_sum[:, h : h + 1])
            nc.gpsimd.tensor_tensor(inv_sum[:, h : h + 1], row_sum[:, h : h + 1], minus_one[:], ALU.pow)

        probs = [sb.tile([P, I], F32, name=f"probs{h}", align_bytes=64)[:] for h in range(HALVES)]
        for h in range(HALVES):
            exponentiate(h)
        gather_plane(1)
        vt_bf[0] = room1.tile([P, I], BF16, name="vt_bf0", offset=4096, align_bytes=256)[:]
        turn_plane(0)
        w_all = room1.tile([P, HALVES * I], BF16, name="w_all", offset=0, align_bytes=256)
        w_bf = [w_all[:, h * I : (h + 1) * I] for h in range(HALVES)]

        def weigh(h):
            nc.vector.scalar_tensor_tensor(w_bf[h], probs[h], inv_sum[:, h : h + 1], size_rows[:], ALU.mult, ALU.mult)

        def turn_weights(h, copy):
            words = w_bf[h].bitcast(F32)
            turn_words([words[:, u * P : (u + 1) * P] for u in range(2)], wt_bf[:, h * P * PACK : (h + 1) * P * PACK], copy)

        def quantise_weights(h):
            nc.vector.quantize_mx(
                out=w_codes[:, h * P : (h + 1) * P].bitcast(FP8X4),
                scales=w_scales[:, h * P : (h + 1) * P],
                in_=wt_bf[:, h * P * PACK : (h + 1) * P * PACK],
            )

        weigh(0)
        weigh(1)
        gather_plane(2)
        early_codes = room2.tile([P, Q + 2 * P], U32, name="early_codes", offset=0, align_bytes=256)
        wt_bf = room2.tile([P, Q * PACK], BF16, name="wt_bf", offset=4096, align_bytes=256)
        vt_bf[1] = room2.tile([P, I], BF16, name="vt_bf1", offset=6144, align_bytes=256)[:]
        vt_bf[2] = sb.tile([P, I], BF16, name="vt_bf2", align_bytes=64)[:]
        w_codes = early_codes[:, :Q]
        v_codes[0] = early_codes[:, Q : Q + P]
        v_codes[1] = early_codes[:, Q + P :]
        quantise_plane(0)
        turn_weights(0, nc.vector.tensor_copy)
        turn_plane(1)
        turn_weights(1, nc.scalar.copy)
        quantise_plane(1)
        quantise_weights(0)
        quantise_weights(1)
        turn_plane(2)

        out_dealt = out_0.rearrange("(p r) q -> p r q", r=PACK)
        acc = [ps.tile([P, PACK, P], F32, name=f"acc{h}", tag=f"bank{h}") for h in range(HALVES)]

        def multiply(r):
            for h in range(HALVES):
                nc.tensor.matmul_mx(
                    out=acc[h][:, r, :],
                    lhsT=v_codes[r].bitcast(FP8X4),
                    lhsT_scale=v_scales[r],
                    rhs=w_codes[:, h * P : (h + 1) * P].bitcast(FP8X4),
                    rhs_scale=w_scales[:, h * P : (h + 1) * P],
                    start=True,
                    stop=True,
                )

        def leave_bank(h, first, end, copy):
            copy(y[:, first:end, h * P : (h + 1) * P], acc[h][:, first:end, :])

        multiply(0)
        multiply(1)
        gather_plane(3)
        y = room3.tile([P, PACK, Q], F32, name="y", offset=0, align_bytes=256)
        late_codes = room3.tile([P, 2 * P], U32, name="late_codes", offset=4096, align_bytes=256)
        v_codes[2] = late_codes[:, :P]
        v_codes[3] = late_codes[:, P:]
        words = vg_bf[3][:].bitcast(F32)
        last_bank = turn.tile([P, 2, P], F32, name="turn_bank")
        for u in range(2):
            nc.tensor.transpose(last_bank[:, u, :], words[:, u::2], ident[:])
        for c in range(2):
            nc.scalar.copy(
                vt_bf[3][:, c * I // 2 : (c + 1) * I // 2].bitcast(F32).rearrange("p (c u) -> p c u", u=2),
                last_bank[:, :, c * P // 2 : (c + 1) * P // 2].rearrange("p u c -> p c u"),
            )
        leave_bank(0, 0, 2, nc.vector.tensor_copy)
        leave_bank(1, 0, 2, nc.scalar.copy)
        quantise_plane(2)
        plane2_out = ps.tile([P, Q], F32, name="plane2_out", tag="bank2")
        nc.tensor.matmul_mx(
            out=plane2_out[:],
            lhsT=v_codes[2].bitcast(FP8X4),
            lhsT_scale=v_scales[2],
            rhs=w_codes.bitcast(FP8X4),
            rhs_scale=w_scales[:],
            start=True,
            stop=True,
        )
        multiply(2)
        for c in range(2):
            cols = slice(c * P // 2, (c + 1) * P // 2)
            nc.vector.quantize_mx(
                out=v_codes[3][:, cols].bitcast(FP8X4),
                scales=v_scales[3][:, cols],
                in_=vt_bf[3][:, c * I // 2 : (c + 1) * I // 2],
            )
        nc.scalar.copy(y[:, 2, :], plane2_out[:])
        nc.sync.dma_start(out_dealt[:, :3, :], y[:, :3, :])
        multiply(3)

        y_bf = sb.tile([P, Q, PACK], BF16, name="y_bf", align_bytes=64)
        y_codes = sb.tile([P, Q], U32, name="y_codes", align_bytes=256)
        y_scales = sb.tile([P, Q], U8, name="y_scales", align_bytes=256)
        nc.vector.tensor_copy(y_bf[:, :P, :], acc[0][:].rearrange("p r q -> p q r"))
        leave_bank(1, 3, PACK, nc.scalar.copy)
        for c in range(2):
            nc.scalar.copy(
                y_bf[:, P + c * P // 2 : P + (c + 1) * P // 2, :],
                acc[1][:, :, c * P // 2 : (c + 1) * P // 2].rearrange("p r q -> p q r"),
            )
        leave_bank(0, 3, PACK, nc.vector.tensor_copy)
        nc.sync.dma_start(out_dealt[:, 3, :], y[:, 3, :])
        for first, end in ((0, P), (P, P + P // 2), (P + P // 2, Q)):
            nc.vector.quantize_mx(
                out=y_codes[:, first:end].bitcast(FP8X4),
                scales=y_scales[:, first:end],
                in_=y_bf[:, first:end, :].rearrange("p q r -> p (q r)"),
            )
        nc.sync.dma_start(out_1[0].rearrange("p c r -> p (c r)").bitcast(I32), y_codes[:].bitcast(I32))

        for quad in range(4):
            queue = nc.scalar if quad == 0 else nc.sync
            queue.dma_start(
                out_2[0][4 * quad : 4 * quad + 4, :].bitcast(I32),
                y_scales[32 * quad : 32 * quad + 4, :].bitcast(I32),
            )
